import numpy as np
import ml_dtypes


def mxq(x, axis, fmt="e4m3"):
    dtype, down = {"e4m3": (ml_dtypes.float8_e4m3fn, 7), "e5m2": (ml_dtypes.float8_e5m2, 14)}[fmt]
    v = np.moveaxis(np.asarray(x, np.float32).astype(ml_dtypes.bfloat16).astype(np.float64), axis, -1)
    blocks = v.reshape(v.shape[:-1] + (-1, 32))
    amax = np.abs(blocks).max(-1, keepdims=True)
    byte = np.maximum(np.where(amax > 0, np.frexp(amax)[1] - 1 + 127, 0) - down, 1)
    scale = np.exp2(byte - 127.0)
    codes = (blocks / scale).astype(np.float32).astype(dtype).astype(np.float64)
    return np.moveaxis((codes * scale).reshape(v.shape), -1, axis)


WIDE = False


def mx_kscale(k):
    if not WIDE:
        return np.ones(k)
    levels = np.array([24, -24, 12, -12, 0])
    if k % 512:
        return np.exp2(np.random.permutation(np.resize(levels, k // 32))).repeat(32)
    a = np.empty((k // 512, 16))
    for p in range(k // 512):
        a[p, :8] = np.random.permutation(np.resize(levels, 8))
        for g in range(8):
            far = levels[np.abs(levels - a[p, g]) >= 10]
            a[p, g + 8] = far[np.random.randint(len(far))]
    return np.exp2(a.ravel()).repeat(32)


def f64(x):
    return np.asarray(x).astype(np.float64)


def striped(idx):
    return np.tile(idx.reshape(-1, 16).T, (8, 1)).astype(np.uint16)


def unstriped(offs):
    return offs[:16].T.reshape(-1).astype(np.int64)


E2M1 = np.array([0.0, 0.5, 1.0, 1.5, 2.0, 3.0, 4.0, 6.0, -0.0, -0.5, -1.0, -1.5, -2.0, -3.0, -4.0, -6.0])


def pack_weight(w, fmt):
    k, n = w.shape
    w = f64(np.asarray(w, np.float32).astype(ml_dtypes.bfloat16)).reshape(k // 32, 32, n)
    amax = np.abs(w).max(1)
    if fmt == "e4m3":
        byte = np.frexp(amax)[1] - 1 + 127 - 7
    else:
        mant, ex = np.frexp(amax / 6.0)
        byte = np.where(mant > 0.5, ex, ex - 1) + 127
    byte = np.clip(np.where(amax > 0, byte, 1), 1, 254)
    scaled = (w * np.exp2(127.0 - byte)[:, None, :]).reshape(k, n).astype(np.float32)
    by_word = np.ascontiguousarray(scaled.reshape(k // 512, 128, 4, n).transpose(0, 1, 3, 2))
    if fmt == "e4m3":
        words = by_word.astype(ml_dtypes.float8_e4m3fn).view(np.uint8)
    else:
        c = by_word.astype(ml_dtypes.float4_e2m1fn).view(np.uint8) & 0xF
        words = (c[..., 0::2] | (c[..., 1::2] << 4)).reshape(k // 512, 128, 2 * n)
    return np.ascontiguousarray(words), np.ascontiguousarray(byte.astype(np.uint8).reshape(k // 512, 16, n))


def unpack_weight(words, scales, fmt):
    g, _, n = scales.shape
    words = np.ascontiguousarray(words).reshape(g, 128, n, -1)
    if fmt == "e4m3":
        vals = words.view(ml_dtypes.float8_e4m3fn).astype(np.float64)
    else:
        nib = np.empty((g, 128, n, 4), np.uint8)
        nib[..., 0::2] = words & 0xF
        nib[..., 1::2] = words >> 4
        vals = E2M1[nib]
    vals = vals * np.repeat(np.exp2(scales.astype(np.float64) - 127.0), 8, axis=1)[..., None]
    return vals.transpose(0, 1, 3, 2).reshape(g * 512, n)


def pack_table4(v):
    words, scales = pack_weight(v, "e2m1")
    g, t = words.shape[0] // 2, v.shape[1]
    return np.ascontiguousarray(words.reshape(g, 2, 128, t, 2).transpose(0, 2, 3, 1, 4).reshape(g, 128, t, 4)), scales


def unpack_table4(words, scales):
    g, _, t, _ = words.shape
    return unpack_weight(words.reshape(g, 128, t, 2, 2).transpose(0, 3, 1, 2, 4).reshape(2 * g, 128, 2 * t), scales, "e2m1")


def sigm(f):
    return 1.0 / (1.0 + np.exp(-np.maximum(f, -700.0)))


K, N, T, J = 1024, 512, 2048, 1024


def setup_inputs():
    n = np.random.standard_normal
    s = mx_kscale(K)[:, None]
    p_tab = pack_table4(n((K, T)) * s)
    p_wa = pack_weight(n((K, N)) / np.sqrt(2 * K) / s, "e4m3")
    return {
        "tab_words": p_tab[0],
        "tab_scales": p_tab[1],
        "wa_words": p_wa[0],
        "wa_scales": p_wa[1],
        "wb": (n((K, N)) / np.sqrt(2 * K) / s).astype(np.float32),
        "wc": (n((K, N)) / np.sqrt(K) / s).astype(np.float32),
        "wgo": np.tile(np.random.uniform(0.5, 2.0, J), (128, 1)).astype(np.float32),
        "offs": striped(np.random.permutation(T)[:J]),
        "offs2": striped(np.random.permutation(T)[:J]),
    }


def reference(tab_words, tab_scales, wa_words, wa_scales, wb, wc, wgo, offs, offs2):
    idx = unstriped(offs)
    idx2 = unstriped(offs2)
    tab_ = unpack_table4(tab_words, tab_scales)[:, idx]
    tabb_ = unpack_table4(tab_words, tab_scales)[:, idx2]
    wa_ = unpack_weight(wa_words, wa_scales, "e4m3")
    wb_ = mxq(f64(wb), 0, "e4m3")
    za = wa_.T @ tabb_ + wb_.T @ tab_
    eta = sigm(za)
    wc_ = mxq(f64(wc), 0, "e4m3")
    ms = wc_.T @ tab_
    out = np.zeros((N, T))
    out[:, idx2] = f64(wgo)[0] * (np.maximum(eta * ms, 0.0))
    return out

@@ -1,0 +1,199 @@
+from contextlib import ExitStack
+
+import concourse.mybir as mybir
+
+K, N, T, J = 1024, 512, 2048, 1024
+FLOPS = 2 * 3 * K * N * J
+
+F32 = mybir.dt.float32
+BF16 = mybir.dt.bfloat16
+I32 = mybir.dt.int32
+U32 = mybir.dt.uint32
+U16 = mybir.dt.uint16
+U8 = mybir.dt.uint8
+FP8X4 = mybir.dt.float8_e4m3fn_x4
+FP4X4 = mybir.dt.float4_e2m1fn_x4
+MULT = mybir.AluOpType.mult
+MAX = mybir.AluOpType.max
+SIGMOID = mybir.ActivationFunctionType.Sigmoid
+
+P = 128
+PACK = 4
+PASSES = 2
+K_PASS = P * PACK
+HALF = 512
+HALVES = J // HALF
+N_TILES = N // P
+LIST_COLS = HALF // 16
+
+
+def tile_list_rgg_relu_kernel(tc, tab_words, tab_scales, wa_words, wa_scales, wb, wc, wgo, offs, offs2, out):
+    nc = tc.nc
+    with ExitStack() as ctx:
+        keep = ctx.enter_context(tc.tile_pool(name="keep", bufs=1))
+        ring = ctx.enter_context(tc.tile_pool(name="ring", bufs=3))
+        psum = ctx.enter_context(tc.psum_pool(name="psum", bufs=4))
+
+        lists = [keep.tile([P, J // 16], U16, name=f"list{i}") for i in range(2)]
+        scale_window = keep.tile([P, T // 4], I32, align_bytes=64)
+        word_window = keep.tile([P, T], I32, align_bytes=64)
+        wa_codes = keep.tile([P, PASSES, N], I32, align_bytes=64)
+        wa_plane = keep.tile([P, PASSES, N // 4], I32, align_bytes=64)
+        picked_scales = [keep.tile([P, J], U8, name=f"picked_scales{i}", align_bytes=64) for i in range(2)]
+        shifted_scales = [keep.tile([P, J // 4], I32, name=f"shifted_scales{i}", align_bytes=64) for i in range(2)]
+        out_windows = [keep.tile([P, T], F32, name=f"out_window{i}", align_bytes=64) for i in range(2)]
+        edge_weight = keep.tile([P, J], F32, align_bytes=64)
+        warm = keep.tile([P, 8], F32)
+
+        nc.vector.memset(scale_window[:], 0)
+        nc.gpsimd.memset(wa_plane[:], 0)
+        nc.vector.memset(warm[:], 0.0)
+        nc.scalar.activation(out=warm[:, 0:1], in_=warm[:, 1:2], func=SIGMOID)
+        for i in range(2):
+            nc.vector.memset(shifted_scales[i][:], 0)
+        for i in range(2):
+            nc.vector.memset(out_windows[i][:], 0.0)
+
+        nc.sync.dma_start(lists[0][:], offs)
+        nc.sync.dma_start(lists[1][:], offs2)
+        for q in range(4):
+            nc.sync.dma_start(
+                out=scale_window[32 * q : 32 * q + 8, :],
+                in_=tab_scales[:, 4 * q : 4 * q + 4, :].bitcast(I32),
+            )
+        for q in range(4):
+            nc.gpsimd.dma_start(
+                out=wa_plane[32 * q : 32 * q + 4, :, :],
+                in_=wa_scales[:, 4 * q : 4 * q + 4, :].bitcast(I32).rearrange("a r c -> r a c"),
+            )
+        nc.sync.dma_start(out=word_window[:], in_=tab_words[0].rearrange("p t b -> p (t b)").bitcast(I32))
+        nc.sync.dma_start(out=wa_codes[:], in_=wa_words.rearrange("a p n i -> p a (n i)").bitcast(I32))
+
+        pieces = [(0, 1), (1, 4)]
+        raw = {}
+        for first, last in pieces:
+            for a in range(PASSES):
+                for w, weight in enumerate((wb, wc)):
+                    t = keep.tile([P, PACK, (last - first) * P], F32, name=f"raw{first}_{w}_{a}")
+                    nc.sync.dma_start(
+                        out=t[:],
+                        in_=weight[a * K_PASS : (a + 1) * K_PASS, first * P : last * P].rearrange("(p i) n -> p i n", i=PACK),
+                    )
+                    for n in range(first, last):
+                        raw[n, w, a] = t[:, :, (n - first) * P : (n - first + 1) * P]
+            if first == 0:
+                nc.sync.dma_start(out=edge_weight[:], in_=wgo)
+
+        grouped = [keep.tile([P, 2, PASSES, P, PACK], BF16, name=f"grouped{n}", align_bytes=64) for n in range(N_TILES)]
+        codes = [keep.tile([P, 2, PASSES, P], U32, name=f"codes{n}", align_bytes=64) for n in range(N_TILES)]
+        planes = [keep.tile([P, 2, PASSES, P], U8, name=f"planes{n}", align_bytes=64) for n in range(N_TILES)]
+
+        def round_weights(n):
+            for a in range(PASSES):
+                for w in range(2):
+                    nc.scalar.copy(
+                        out=grouped[n][:, w, a].rearrange("p (c m) i -> p c i m", m=4),
+                        in_=raw[n, w, a].rearrange("p i (c m) -> p c i m", m=4),
+                    )
+
+        def quantize_weights(n):
+            nc.vector.quantize_mx(
+                out=codes[n][:].rearrange("p w a n -> p (w a n)").bitcast(FP8X4),
+                scales=planes[n][:].rearrange("p w a n -> p (w a n)"),
+                in_=grouped[n][:].rearrange("p w a n i -> p (w a n i)"),
+            )
+
+        def pick_scales(i):
+            nc.vector.tensor_copy(out=picked_scales[i][:], in_=scale_window[:].bitcast(U8).indirect(lists[i][:]))
+            nc.gpsimd.dma_start(out=shifted_scales[i][0:100, :], in_=picked_scales[i][4:104, :].bitcast(I32))
+
+        picked = {}
+        parted = {}
+
+        def pick_words(i, h):
+            picked[i, h] = keep.tile([P, HALF], U32, name=f"picked{i}_{h}", align_bytes=64)
+            nc.vector.tensor_copy(
+                out=picked[i, h][:],
+                in_=word_window[:].bitcast(U32).indirect(lists[i][:, h * LIST_COLS : (h + 1) * LIST_COLS]),
+            )
+
+        def part_words(i, h):
+            parted[i, h] = keep.tile([P, PASSES, 2 * HALF], U8, name=f"parted{i}_{h}", align_bytes=64)
+            nc.vector.tensor_copy(
+                out=parted[i, h][:].bitcast(U16),
+                in_=picked[i, h][:].bitcast(U16).rearrange("p (j d) -> p d j", d=PASSES),
+            )
+
+        def table_operand(i, h, a):
+            cols = slice(h * HALF, (h + 1) * HALF)
+            plane = picked_scales[i][:, cols] if a == 0 else shifted_scales[i][:].bitcast(U8)[:, cols]
+            return parted[i, h][:, a, :].bitcast(FP4X4), plane
+
+        message = {}
+
+        def multiply(n, h):
+            cols = slice(n * P, (n + 1) * P)
+            za = psum.tile([P, HALF], F32, name="za")
+            ms = psum.tile([P, HALF], F32, name="ms")
+            for a in range(PASSES):
+                words, plane = table_operand(1, h, a)
+                nc.tensor.matmul_mx(
+                    out=za[:], lhsT=wa_codes[:, a, cols].bitcast(FP8X4), lhsT_scale=wa_plane[:, a, :].bitcast(U8)[:, cols],
+                    rhs=words, rhs_scale=plane, start=(a == 0), stop=False,
+                )
+            for a in range(PASSES):
+                words, plane = table_operand(0, h, a)
+                nc.tensor.matmul_mx(
+                    out=za[:], lhsT=codes[n][:, 0, a, :].bitcast(FP8X4), lhsT_scale=planes[n][:, 0, a, :],
+                    rhs=words, rhs_scale=plane, start=False, stop=(a == PASSES - 1),
+                )
+            for a in range(PASSES):
+                words, plane = table_operand(0, h, a)
+                nc.tensor.matmul_mx(
+                    out=ms[:], lhsT=codes[n][:, 1, a, :].bitcast(FP8X4), lhsT_scale=planes[n][:, 1, a, :],
+                    rhs=words, rhs_scale=plane, start=(a == 0), stop=(a == PASSES - 1),
+                )
+            eta = ring.tile([P, HALF], F32, name="eta")
+            nc.scalar.activation(out=eta[:], in_=za[:], func=SIGMOID)
+            return ms, eta
+
+        def gate(n, h, ms, eta):
+            message[n, h] = ring.tile([P, HALF], F32, name="message")
+            nc.vector.scalar_tensor_tensor(out=message[n, h][:], in0=ms[:], scalar=0.0, in1=eta[:], op0=MAX, op1=MULT)
+
+        def scatter(n, h):
+            window = out_windows[n % 2]
+            nc.vector.tensor_tensor(
+                window[:].indirect(lists[1][:, h * LIST_COLS : (h + 1) * LIST_COLS]),
+                message[n, h][:],
+                edge_weight[:, h * HALF : (h + 1) * HALF],
+                MULT,
+            )
+            if h == HALVES - 1:
+                nc.sync.dma_start(out=out[n * P : (n + 1) * P, :], in_=window[:])
+
+        pick_scales(1)
+        pick_scales(0)
+        pick_words(1, 0)
+        pick_words(0, 0)
+        part_words(1, 0)
+        part_words(0, 0)
+        round_weights(0)
+        quantize_weights(0)
+        sums = {(0, 0): multiply(0, 0)}
+        pick_words(1, 1)
+        pick_words(0, 1)
+        part_words(1, 1)
+        part_words(0, 1)
+        sums[0, 1] = multiply(0, 1)
+        gate(0, 0, *sums[0, 0])
+        units = [(n, h) for n in range(N_TILES) for h in range(HALVES)]
+        for u, (n, h) in enumerate(units):
+            if h == 0 and n + 1 < N_TILES:
+                round_weights(n + 1)
+                quantize_weights(n + 1)
+            if u + 2 < len(units):
+                sums[units[u + 2]] = multiply(*units[u + 2])
+            if u + 1 < len(units):
+                gate(*units[u + 1], *sums[units[u + 1]])
+            scatter(n, h)

@@ -1,6 +1,7 @@
 from contextlib import ExitStack
 
 import concourse.mybir as mybir
+from concourse.masks import make_identity
 
 K, N, T, J = 1024, 512, 2048, 1024
 FLOPS = 2 * 3 * K * N * J
@@ -14,8 +15,9 @@ U8 = mybir.dt.uint8
 FP8X4 = mybir.dt.float8_e4m3fn_x4
 FP4X4 = mybir.dt.float4_e2m1fn_x4
 MULT = mybir.AluOpType.mult
-MAX = mybir.AluOpType.max
 SIGMOID = mybir.ActivationFunctionType.Sigmoid
+RELU = mybir.ActivationFunctionType.Relu
+COPY = mybir.ActivationFunctionType.Copy
 
 P = 128
 PACK = 4
@@ -24,7 +26,9 @@ K_PASS = P * PACK
 HALF = 512
 HALVES = J // HALF
 N_TILES = N // P
+E_TILES = HALF // P
 LIST_COLS = HALF // 16
+KIB = 1024
 
 
 def tile_list_rgg_relu_kernel(tc, tab_words, tab_scales, wa_words, wa_scales, wb, wc, wgo, offs, offs2, out):
@@ -32,168 +36,207 @@ def tile_list_rgg_relu_kernel(tc, tab_words, tab_scales, wa_words, wa_scales, wb
     with ExitStack() as ctx:
         keep = ctx.enter_context(tc.tile_pool(name="keep", bufs=1))
         ring = ctx.enter_context(tc.tile_pool(name="ring", bufs=3))
-        psum = ctx.enter_context(tc.psum_pool(name="psum", bufs=4))
+        relay = ctx.enter_context(tc.tile_pool(name="relay", bufs=1))
+        psum = ctx.enter_context(tc.psum_pool(name="psum", bufs=3))
+        turn = ctx.enter_context(tc.psum_pool(name="turn", bufs=2))
+
+        def placed(name, shape, dtype, kib):
+            return relay.tile(shape, dtype, name=name, offset=kib * KIB, align_bytes=64)
+
+        picked_words_at = {(1, 0): 0, (0, 0): 2, (1, 1): 2, (0, 1): 4}
+        picked_scales_at = {0: 8, 1: 0}
+        codes_at = {(0, 0): 1, (2, 0): 1, (0, 1): 6, (2, 1): 6, (1, 0): 2, (3, 0): 2, (1, 1): 4, (3, 1): 4}
+        weighted_at = {0: 11, 1: 15, 2: 18}
+        grouped_at = {(0, 0): 4, (0, 1): 20, (1, 0): 22, (1, 1): 10, (2, 0): 12, (2, 1): 14, (3, 0): 16, (3, 1): 18}
 
         lists = [keep.tile([P, J // 16], U16, name=f"list{i}") for i in range(2)]
-        scale_window = keep.tile([P, T // 4], I32, align_bytes=64)
+        scale_window = placed("scale_window", [P, T // 4], I32, 6)
         word_window = keep.tile([P, T], I32, align_bytes=64)
         wa_codes = keep.tile([P, PASSES, N], I32, align_bytes=64)
         wa_plane = keep.tile([P, PASSES, N // 4], I32, align_bytes=64)
-        picked_scales = [keep.tile([P, J], U8, name=f"picked_scales{i}", align_bytes=64) for i in range(2)]
-        shifted_scales = [keep.tile([P, J // 4], I32, name=f"shifted_scales{i}", align_bytes=64) for i in range(2)]
+        shifted_scales = [keep.tile([P, 2, HALF // 4], I32, name=f"shifted_scales{h}", align_bytes=64) for h in range(HALVES)]
         out_windows = [keep.tile([P, T], F32, name=f"out_window{i}", align_bytes=64) for i in range(2)]
-        edge_weight = keep.tile([P, J], F32, align_bytes=64)
+        weight_rows = keep.tile([P, P], F32, align_bytes=64)
+        edge_weight = keep.tile([P, J // P], F32)
+        identity = keep.tile([P, P], F32, align_bytes=64)
+        planes = keep.tile([P, N_TILES, 2, PASSES, P], U8, align_bytes=64)
         warm = keep.tile([P, 8], F32)
 
-        nc.vector.memset(scale_window[:], 0)
-        nc.gpsimd.memset(wa_plane[:], 0)
-        nc.vector.memset(warm[:], 0.0)
+        nc.gpsimd.memset(scale_window[:], 0)
+        nc.gpsimd.memset(warm[:], 0.0)
         nc.scalar.activation(out=warm[:, 0:1], in_=warm[:, 1:2], func=SIGMOID)
-        for i in range(2):
-            nc.vector.memset(shifted_scales[i][:], 0)
-        for i in range(2):
-            nc.vector.memset(out_windows[i][:], 0.0)
+        nc.gpsimd.memset(wa_plane[:], 0)
+        nc.gpsimd.memset(shifted_scales[0][:], 0)
+        nc.gpsimd.memset(weight_rows[:], 0.0)
+        make_identity(nc, identity[:])
+        nc.gpsimd.memset(shifted_scales[1][:], 0)
+        nc.gpsimd.memset(out_windows[0][:], 0.0)
+        nc.gpsimd.memset(out_windows[1][:], 0.0)
 
-        nc.sync.dma_start(lists[0][:], offs)
+        raw = {}
+
+        def load_weight(w, first, last):
+            for a in range(PASSES):
+                t = keep.tile([P, PACK, (last - first) * P], F32, name=f"raw{first}_{w}_{a}")
+                nc.sync.dma_start(
+                    out=t[:],
+                    in_=(wb, wc)[w][a * K_PASS : (a + 1) * K_PASS, first * P : last * P].rearrange("(p i) n -> p i n", i=PACK),
+                )
+                for n in range(first, last):
+                    raw[n, w, a] = t[:, :, (n - first) * P : (n - first + 1) * P]
+
         nc.sync.dma_start(lists[1][:], offs2)
+        nc.sync.dma_start(lists[0][:], offs)
         for q in range(4):
             nc.sync.dma_start(
                 out=scale_window[32 * q : 32 * q + 8, :],
                 in_=tab_scales[:, 4 * q : 4 * q + 4, :].bitcast(I32),
             )
+        nc.sync.dma_start(out=word_window[:], in_=tab_words[0].rearrange("p t b -> p (t b)").bitcast(I32))
+        load_weight(0, 0, 2)
+        nc.sync.dma_start(out=wa_codes[:], in_=wa_words.rearrange("a p n i -> p a (n i)").bitcast(I32))
         for q in range(4):
-            nc.gpsimd.dma_start(
+            nc.sync.dma_start(
                 out=wa_plane[32 * q : 32 * q + 4, :, :],
                 in_=wa_scales[:, 4 * q : 4 * q + 4, :].bitcast(I32).rearrange("a r c -> r a c"),
             )
-        nc.sync.dma_start(out=word_window[:], in_=tab_words[0].rearrange("p t b -> p (t b)").bitcast(I32))
-        nc.sync.dma_start(out=wa_codes[:], in_=wa_words.rearrange("a p n i -> p a (n i)").bitcast(I32))
+        nc.sync.dma_start(out=weight_rows[0 : J // P, :], in_=wgo[0].rearrange("(c p) -> c p", p=P))
+        load_weight(1, 0, 2)
+        load_weight(0, 2, 4)
+        load_weight(1, 2, 4)
 
-        pieces = [(0, 1), (1, 4)]
-        raw = {}
-        for first, last in pieces:
-            for a in range(PASSES):
-                for w, weight in enumerate((wb, wc)):
-                    t = keep.tile([P, PACK, (last - first) * P], F32, name=f"raw{first}_{w}_{a}")
-                    nc.sync.dma_start(
-                        out=t[:],
-                        in_=weight[a * K_PASS : (a + 1) * K_PASS, first * P : last * P].rearrange("(p i) n -> p i n", i=PACK),
-                    )
-                    for n in range(first, last):
-                        raw[n, w, a] = t[:, :, (n - first) * P : (n - first + 1) * P]
-            if first == 0:
-                nc.sync.dma_start(out=edge_weight[:], in_=wgo)
+        turned_rows = turn.tile([P, HALF], F32, name="turned")
+        nc.tensor.transpose(turned_rows[:, 0:P], weight_rows[:], identity[:])
+        nc.scalar.copy(out=edge_weight[:], in_=turned_rows[:, 0 : J // P])
 
-        grouped = [keep.tile([P, 2, PASSES, P, PACK], BF16, name=f"grouped{n}", align_bytes=64) for n in range(N_TILES)]
-        codes = [keep.tile([P, 2, PASSES, P], U32, name=f"codes{n}", align_bytes=64) for n in range(N_TILES)]
-        planes = [keep.tile([P, 2, PASSES, P], U8, name=f"planes{n}", align_bytes=64) for n in range(N_TILES)]
-
-        def round_weights(n):
-            for a in range(PASSES):
-                for w in range(2):
-                    nc.scalar.copy(
-                        out=grouped[n][:, w, a].rearrange("p (c m) i -> p c i m", m=4),
-                        in_=raw[n, w, a].rearrange("p i (c m) -> p c i m", m=4),
-                    )
-
-        def quantize_weights(n):
-            nc.vector.quantize_mx(
-                out=codes[n][:].rearrange("p w a n -> p (w a n)").bitcast(FP8X4),
-                scales=planes[n][:].rearrange("p w a n -> p (w a n)"),
-                in_=grouped[n][:].rearrange("p w a n i -> p (w a n i)"),
-            )
-
-        def pick_scales(i):
-            nc.vector.tensor_copy(out=picked_scales[i][:], in_=scale_window[:].bitcast(U8).indirect(lists[i][:]))
-            nc.gpsimd.dma_start(out=shifted_scales[i][0:100, :], in_=picked_scales[i][4:104, :].bitcast(I32))
-
-        picked = {}
+        grouped = {}
+        codes = {}
+        picked_scales = {}
+        picked_words = {}
         parted = {}
 
-        def pick_words(i, h):
-            picked[i, h] = keep.tile([P, HALF], U32, name=f"picked{i}_{h}", align_bytes=64)
-            nc.vector.tensor_copy(
-                out=picked[i, h][:],
-                in_=word_window[:].bitcast(U32).indirect(lists[i][:, h * LIST_COLS : (h + 1) * LIST_COLS]),
+        def round_weights(n, w):
+            grouped[n, w] = placed(f"grouped{n}_{w}", [P, PASSES, P, PACK], BF16, grouped_at[n, w])
+            for a in range(PASSES):
+                nc.scalar.copy(
+                    out=grouped[n, w][:, a].rearrange("p (c m) i -> p c i m", m=4),
+                    in_=raw[n, w, a].rearrange("p i (c m) -> p c i m", m=4),
+                )
+
+        def quantize_weights(n, w):
+            codes[n, w] = placed(f"codes{n}_{w}", [P, PASSES, P], U32, codes_at[n, w])
+            nc.vector.quantize_mx(
+                out=codes[n, w][:].rearrange("p a n -> p (a n)").bitcast(FP8X4),
+                scales=planes[:, n, w].rearrange("p a n -> p (a n)"),
+                in_=grouped[n, w][:].rearrange("p a n i -> p (a n i)"),
             )
+
+        def list_half(i, h):
+            return lists[i][:, h * LIST_COLS : (h + 1) * LIST_COLS]
+
+        def pick_scales(h, queue):
+            picked_scales[h] = placed(f"picked_scales{h}", [P, 2, HALF], U8, picked_scales_at[h])
+            for i in (1, 0):
+                nc.vector.tensor_copy(out=picked_scales[h][:, i, :], in_=scale_window[:].bitcast(U8).indirect(list_half(i, h)))
+            queue.dma_start(out=shifted_scales[h][0:100], in_=picked_scales[h][4:104].bitcast(I32))
+
+        def pick_words(i, h):
+            picked_words[i, h] = placed(f"picked_words{i}_{h}", [P, HALF], U32, picked_words_at[i, h])
+            nc.vector.tensor_copy(out=picked_words[i, h][:], in_=word_window[:].bitcast(U32).indirect(list_half(i, h)))
 
         def part_words(i, h):
             parted[i, h] = keep.tile([P, PASSES, 2 * HALF], U8, name=f"parted{i}_{h}", align_bytes=64)
             nc.vector.tensor_copy(
                 out=parted[i, h][:].bitcast(U16),
-                in_=picked[i, h][:].bitcast(U16).rearrange("p (j d) -> p d j", d=PASSES),
+                in_=picked_words[i, h][:].bitcast(U16).rearrange("p (j d) -> p d j", d=PASSES),
             )
 
-        def table_operand(i, h, a):
-            cols = slice(h * HALF, (h + 1) * HALF)
-            plane = picked_scales[i][:, cols] if a == 0 else shifted_scales[i][:].bitcast(U8)[:, cols]
-            return parted[i, h][:, a, :].bitcast(FP4X4), plane
+        def table_operand(i, h, a, first, width):
+            cols = slice(first, first + width)
+            plane = picked_scales[h][:, i, cols] if a == 0 else shifted_scales[h][:, i, :].bitcast(U8)[:, cols]
+            return parted[i, h][:, a, 2 * first : 2 * (first + width)].bitcast(FP4X4), plane
 
-        message = {}
-
-        def multiply(n, h):
+        def weighted_gate(n, h):
             cols = slice(n * P, (n + 1) * P)
-            za = psum.tile([P, HALF], F32, name="za")
+            zt = psum.tile([P, E_TILES, P], F32, name="zt")
+            for e in range(E_TILES):
+                for a in range(PASSES):
+                    words, plane = table_operand(1, h, a, e * P, P)
+                    nc.tensor.matmul_mx(
+                        out=zt[:, e, :], lhsT=words, lhsT_scale=plane,
+                        rhs=wa_codes[:, a, cols].bitcast(FP8X4), rhs_scale=wa_plane[:, a, :].bitcast(U8)[:, cols],
+                        start=(a == 0), stop=False,
+                    )
+                    words, plane = table_operand(0, h, a, e * P, P)
+                    nc.tensor.matmul_mx(
+                        out=zt[:, e, :], lhsT=words, lhsT_scale=plane,
+                        rhs=codes[n, 0][:, a, :].bitcast(FP8X4), rhs_scale=planes[:, n, 0, a, :],
+                        start=False, stop=(a == PASSES - 1),
+                    )
+            eta = ring.tile([P, E_TILES, P], F32, name="eta")
+            nc.scalar.activation(out=eta[:], in_=zt[:], func=SIGMOID)
+            u = HALVES * n + h
+            if u in weighted_at:
+                weighted = placed(f"weighted{u}", [P, E_TILES, P], F32, weighted_at[u])
+            else:
+                weighted = ring.tile([P, E_TILES, P], F32, name="weighted", align_bytes=64)
+            for e in range(E_TILES):
+                c = h * E_TILES + e
+                nc.scalar.activation(out=weighted[:, e, :], in_=eta[:, e, :], func=COPY, scale=edge_weight[:, c : c + 1])
+            return weighted
+
+        def messages(n, h):
             ms = psum.tile([P, HALF], F32, name="ms")
             for a in range(PASSES):
-                words, plane = table_operand(1, h, a)
+                words, plane = table_operand(0, h, a, 0, HALF)
                 nc.tensor.matmul_mx(
-                    out=za[:], lhsT=wa_codes[:, a, cols].bitcast(FP8X4), lhsT_scale=wa_plane[:, a, :].bitcast(U8)[:, cols],
-                    rhs=words, rhs_scale=plane, start=(a == 0), stop=False,
-                )
-            for a in range(PASSES):
-                words, plane = table_operand(0, h, a)
-                nc.tensor.matmul_mx(
-                    out=za[:], lhsT=codes[n][:, 0, a, :].bitcast(FP8X4), lhsT_scale=planes[n][:, 0, a, :],
-                    rhs=words, rhs_scale=plane, start=False, stop=(a == PASSES - 1),
-                )
-            for a in range(PASSES):
-                words, plane = table_operand(0, h, a)
-                nc.tensor.matmul_mx(
-                    out=ms[:], lhsT=codes[n][:, 1, a, :].bitcast(FP8X4), lhsT_scale=planes[n][:, 1, a, :],
+                    out=ms[:], lhsT=codes[n, 1][:, a, :].bitcast(FP8X4), lhsT_scale=planes[:, n, 1, a, :],
                     rhs=words, rhs_scale=plane, start=(a == 0), stop=(a == PASSES - 1),
                 )
-            eta = ring.tile([P, HALF], F32, name="eta")
-            nc.scalar.activation(out=eta[:], in_=za[:], func=SIGMOID)
-            return ms, eta
+            message = ring.tile([P, HALF], F32, name="message")
+            nc.scalar.activation(out=message[:], in_=ms[:], func=RELU)
+            return message
 
-        def gate(n, h, ms, eta):
-            message[n, h] = ring.tile([P, HALF], F32, name="message")
-            nc.vector.scalar_tensor_tensor(out=message[n, h][:], in0=ms[:], scalar=0.0, in1=eta[:], op0=MAX, op1=MULT)
+        def turn_gate(weighted):
+            turned = turn.tile([P, HALF], F32, name="turned")
+            for e in range(E_TILES):
+                nc.tensor.transpose(turned[:, e * P : (e + 1) * P], weighted[:, e, :], identity[:])
+            gate = ring.tile([P, HALF], F32, name="gate")
+            nc.scalar.copy(out=gate[:], in_=turned[:])
+            return gate
 
-        def scatter(n, h):
+        def scatter(n, h, gate, message):
             window = out_windows[n % 2]
-            nc.vector.tensor_tensor(
-                window[:].indirect(lists[1][:, h * LIST_COLS : (h + 1) * LIST_COLS]),
-                message[n, h][:],
-                edge_weight[:, h * HALF : (h + 1) * HALF],
-                MULT,
-            )
+            nc.vector.tensor_tensor(window[:].indirect(list_half(1, h)), message[:], gate[:], MULT)
             if h == HALVES - 1:
                 nc.sync.dma_start(out=out[n * P : (n + 1) * P, :], in_=window[:])
 
-        pick_scales(1)
-        pick_scales(0)
+        pick_scales(0, nc.scalar)
         pick_words(1, 0)
         pick_words(0, 0)
         part_words(1, 0)
         part_words(0, 0)
-        round_weights(0)
-        quantize_weights(0)
-        sums = {(0, 0): multiply(0, 0)}
+        round_weights(0, 0)
+        quantize_weights(0, 0)
+        weighted = weighted_gate(0, 0)
+        pick_scales(1, nc.gpsimd)
+        round_weights(0, 1)
+        round_weights(1, 0)
         pick_words(1, 1)
+        quantize_weights(0, 1)
         pick_words(0, 1)
         part_words(1, 1)
         part_words(0, 1)
-        sums[0, 1] = multiply(0, 1)
-        gate(0, 0, *sums[0, 0])
+        rounded_at = {0: [(1, 1), (2, 0)], 1: [(2, 1), (3, 0)], 2: [(3, 1)]}
+        quantized_at = {0: [(1, 0), (1, 1)], 1: [(2, 0)], 2: [(2, 1)], 3: [(3, 0)], 4: [(3, 1)]}
         units = [(n, h) for n in range(N_TILES) for h in range(HALVES)]
         for u, (n, h) in enumerate(units):
-            if h == 0 and n + 1 < N_TILES:
-                round_weights(n + 1)
-                quantize_weights(n + 1)
-            if u + 2 < len(units):
-                sums[units[u + 2]] = multiply(*units[u + 2])
+            gate = turn_gate(weighted)
+            message = messages(n, h)
             if u + 1 < len(units):
-                gate(*units[u + 1], *sums[units[u + 1]])
-            scatter(n, h)
+                weighted = weighted_gate(*units[u + 1])
+            for key in rounded_at.get(u, []):
+                round_weights(*key)
+            for key in quantized_at.get(u, []):
+                quantize_weights(*key)
+            scatter(n, h, gate, message)

@@ -29,6 +29,7 @@ N_TILES = N // P
 E_TILES = HALF // P
 LIST_COLS = HALF // 16
 KIB = 1024
+EDGE = 64
 
 
 def tile_list_rgg_relu_kernel(tc, tab_words, tab_scales, wa_words, wa_scales, wb, wc, wgo, offs, offs2, out):
@@ -40,38 +41,44 @@ def tile_list_rgg_relu_kernel(tc, tab_words, tab_scales, wa_words, wa_scales, wb
         psum = ctx.enter_context(tc.psum_pool(name="psum", bufs=3))
         turn = ctx.enter_context(tc.psum_pool(name="turn", bufs=2))
 
-        def placed(name, shape, dtype, kib):
-            return relay.tile(shape, dtype, name=name, offset=kib * KIB, align_bytes=64)
+        def placed(name, shape, dtype, at):
+            return relay.tile(shape, dtype, name=name, offset=at, align_bytes=64)
 
-        picked_words_at = {(1, 0): 0, (0, 0): 2, (1, 1): 2, (0, 1): 4}
-        picked_scales_at = {0: 8, 1: 0}
-        codes_at = {(0, 0): 1, (2, 0): 1, (0, 1): 6, (2, 1): 6, (1, 0): 2, (3, 0): 2, (1, 1): 4, (3, 1): 4}
-        weighted_at = {0: 11, 1: 15, 2: 18}
-        grouped_at = {(0, 0): 4, (0, 1): 20, (1, 0): 22, (1, 1): 10, (2, 0): 12, (2, 1): 14, (3, 0): 16, (3, 1): 18}
+        picked_words_at = {(1, 0): 0, (0, 0): 2, (1, 1): 4, (0, 1): 6}
+        picked_scales_at = {0: 18, 1: 8}
+        parted_at = {(1, 0): 19 * KIB, (0, 0): 21 * KIB, (1, 1): 23 * KIB + EDGE, (0, 1): 27 * KIB - EDGE}
+        codes_at = {(0, 0): 0, (1, 0): 2}
+        weighted_at = {1: 29, 2: 31, 3: 33, 4: 35}
+        grouped_at = {(0, 0): 37, (0, 1): 25, (1, 0): 4, (1, 1): 39, (2, 0): 29, (2, 1): 31, (3, 0): 33, (3, 1): 35}
+        window_at = {0: 48, 1: 9, 2: 40}
 
         lists = [keep.tile([P, J // 16], U16, name=f"list{i}") for i in range(2)]
-        scale_window = placed("scale_window", [P, T // 4], I32, 6)
+        scale_window = keep.tile([P, T // 4], I32, align_bytes=64)
         word_window = keep.tile([P, T], I32, align_bytes=64)
         wa_codes = keep.tile([P, PASSES, N], I32, align_bytes=64)
         wa_plane = keep.tile([P, PASSES, N // 4], I32, align_bytes=64)
         shifted_scales = [keep.tile([P, 2, HALF // 4], I32, name=f"shifted_scales{h}", align_bytes=64) for h in range(HALVES)]
-        out_windows = [keep.tile([P, T], F32, name=f"out_window{i}", align_bytes=64) for i in range(2)]
+        out_windows = {}
         weight_rows = keep.tile([P, P], F32, align_bytes=64)
         edge_weight = keep.tile([P, J // P], F32)
         identity = keep.tile([P, P], F32, align_bytes=64)
         planes = keep.tile([P, N_TILES, 2, PASSES, P], U8, align_bytes=64)
         warm = keep.tile([P, 8], F32)
 
+        def clear_window(i):
+            out_windows[i] = placed(f"out_window{i}", [P, T], F32, window_at[i] * KIB)
+            nc.gpsimd.memset(out_windows[i][:], 0.0)
+
         nc.gpsimd.memset(scale_window[:], 0)
         nc.gpsimd.memset(warm[:], 0.0)
         nc.scalar.activation(out=warm[:, 0:1], in_=warm[:, 1:2], func=SIGMOID)
-        nc.gpsimd.memset(wa_plane[:], 0)
         nc.gpsimd.memset(shifted_scales[0][:], 0)
+        clear_window(0)
         nc.gpsimd.memset(weight_rows[:], 0.0)
+        nc.gpsimd.memset(wa_plane[:], 0)
+        nc.gpsimd.dma_start(out=weight_rows[0 : J // P, :], in_=wgo[0].rearrange("(c p) -> c p", p=P))
         make_identity(nc, identity[:])
         nc.gpsimd.memset(shifted_scales[1][:], 0)
-        nc.gpsimd.memset(out_windows[0][:], 0.0)
-        nc.gpsimd.memset(out_windows[1][:], 0.0)
 
         raw = {}
 
@@ -96,11 +103,10 @@ def tile_list_rgg_relu_kernel(tc, tab_words, tab_scales, wa_words, wa_scales, wb
         load_weight(0, 0, 2)
         nc.sync.dma_start(out=wa_codes[:], in_=wa_words.rearrange("a p n i -> p a (n i)").bitcast(I32))
         for q in range(4):
-            nc.sync.dma_start(
+            nc.scalar.dma_start(
                 out=wa_plane[32 * q : 32 * q + 4, :, :],
                 in_=wa_scales[:, 4 * q : 4 * q + 4, :].bitcast(I32).rearrange("a r c -> r a c"),
             )
-        nc.sync.dma_start(out=weight_rows[0 : J // P, :], in_=wgo[0].rearrange("(c p) -> c p", p=P))
         load_weight(1, 0, 2)
         load_weight(0, 2, 4)
         load_weight(1, 2, 4)
@@ -116,36 +122,41 @@ def tile_list_rgg_relu_kernel(tc, tab_words, tab_scales, wa_words, wa_scales, wb
         parted = {}
 
         def round_weights(n, w):
-            grouped[n, w] = placed(f"grouped{n}_{w}", [P, PASSES, P, PACK], BF16, grouped_at[n, w])
+            width = PASSES * K_PASS * (3 if (n, w) == (1, 0) else 1)
+            flat = placed(f"grouped{n}_{w}", [P, width], BF16, grouped_at[n, w] * KIB)[:, 0 : PASSES * K_PASS]
+            grouped[n, w] = flat
             for a in range(PASSES):
                 nc.scalar.copy(
-                    out=grouped[n, w][:, a].rearrange("p (c m) i -> p c i m", m=4),
+                    out=flat[:, a * K_PASS : (a + 1) * K_PASS].rearrange("p (c m i) -> p c i m", m=4, i=PACK),
                     in_=raw[n, w, a].rearrange("p i (c m) -> p c i m", m=4),
                 )
 
         def quantize_weights(n, w):
-            codes[n, w] = placed(f"codes{n}_{w}", [P, PASSES, P], U32, codes_at[n, w])
+            if (n, w) in codes_at:
+                codes[n, w] = placed(f"codes{n}_{w}", [P, PASSES, P], U32, codes_at[n, w] * KIB)
+            else:
+                codes[n, w] = keep.tile([P, PASSES, P], U32, name=f"codes{n}_{w}", align_bytes=64)
             nc.vector.quantize_mx(
                 out=codes[n, w][:].rearrange("p a n -> p (a n)").bitcast(FP8X4),
                 scales=planes[:, n, w].rearrange("p a n -> p (a n)"),
-                in_=grouped[n, w][:].rearrange("p a n i -> p (a n i)"),
+                in_=grouped[n, w],
             )
 
         def list_half(i, h):
             return lists[i][:, h * LIST_COLS : (h + 1) * LIST_COLS]
 
         def pick_scales(h, queue):
-            picked_scales[h] = placed(f"picked_scales{h}", [P, 2, HALF], U8, picked_scales_at[h])
+            picked_scales[h] = placed(f"picked_scales{h}", [P, 2, HALF], U8, picked_scales_at[h] * KIB)
             for i in (1, 0):
                 nc.vector.tensor_copy(out=picked_scales[h][:, i, :], in_=scale_window[:].bitcast(U8).indirect(list_half(i, h)))
             queue.dma_start(out=shifted_scales[h][0:100], in_=picked_scales[h][4:104].bitcast(I32))
 
         def pick_words(i, h):
-            picked_words[i, h] = placed(f"picked_words{i}_{h}", [P, HALF], U32, picked_words_at[i, h])
+            picked_words[i, h] = placed(f"picked_words{i}_{h}", [P, HALF], U32, picked_words_at[i, h] * KIB)
             nc.vector.tensor_copy(out=picked_words[i, h][:], in_=word_window[:].bitcast(U32).indirect(list_half(i, h)))
 
         def part_words(i, h):
-            parted[i, h] = keep.tile([P, PASSES, 2 * HALF], U8, name=f"parted{i}_{h}", align_bytes=64)
+            parted[i, h] = placed(f"parted{i}_{h}", [P, PASSES, 2 * HALF], U8, parted_at[i, h])
             nc.vector.tensor_copy(
                 out=parted[i, h][:].bitcast(U16),
                 in_=picked_words[i, h][:].bitcast(U16).rearrange("p (j d) -> p d j", d=PASSES),
@@ -156,7 +167,7 @@ def tile_list_rgg_relu_kernel(tc, tab_words, tab_scales, wa_words, wa_scales, wb
             plane = picked_scales[h][:, i, cols] if a == 0 else shifted_scales[h][:, i, :].bitcast(U8)[:, cols]
             return parted[i, h][:, a, 2 * first : 2 * (first + width)].bitcast(FP4X4), plane
 
-        def weighted_gate(n, h):
+        def weighted_gate(u, n, h):
             cols = slice(n * P, (n + 1) * P)
             zt = psum.tile([P, E_TILES, P], F32, name="zt")
             for e in range(E_TILES):
@@ -175,9 +186,8 @@ def tile_list_rgg_relu_kernel(tc, tab_words, tab_scales, wa_words, wa_scales, wb
                     )
             eta = ring.tile([P, E_TILES, P], F32, name="eta")
             nc.scalar.activation(out=eta[:], in_=zt[:], func=SIGMOID)
-            u = HALVES * n + h
             if u in weighted_at:
-                weighted = placed(f"weighted{u}", [P, E_TILES, P], F32, weighted_at[u])
+                weighted = placed(f"weighted{u}", [P, E_TILES, P], F32, weighted_at[u] * KIB)
             else:
                 weighted = ring.tile([P, E_TILES, P], F32, name="weighted", align_bytes=64)
             for e in range(E_TILES):
@@ -206,7 +216,7 @@ def tile_list_rgg_relu_kernel(tc, tab_words, tab_scales, wa_words, wa_scales, wb
             return gate
 
         def scatter(n, h, gate, message):
-            window = out_windows[n % 2]
+            window = out_windows[n % 3]
             nc.vector.tensor_tensor(window[:].indirect(list_half(1, h)), message[:], gate[:], MULT)
             if h == HALVES - 1:
                 nc.sync.dma_start(out=out[n * P : (n + 1) * P, :], in_=window[:])
@@ -218,25 +228,29 @@ def tile_list_rgg_relu_kernel(tc, tab_words, tab_scales, wa_words, wa_scales, wb
         part_words(0, 0)
         round_weights(0, 0)
         quantize_weights(0, 0)
-        weighted = weighted_gate(0, 0)
-        pick_scales(1, nc.gpsimd)
-        round_weights(0, 1)
         round_weights(1, 0)
+        quantize_weights(1, 0)
+        clear_window(1)
+        round_weights(0, 1)
+        weighted = weighted_gate(0, 0, 0)
+        pick_scales(1, nc.scalar)
         pick_words(1, 1)
-        quantize_weights(0, 1)
         pick_words(0, 1)
+        quantize_weights(0, 1)
         part_words(1, 1)
         part_words(0, 1)
-        rounded_at = {0: [(1, 1), (2, 0)], 1: [(2, 1), (3, 0)], 2: [(3, 1)]}
-        quantized_at = {0: [(1, 0), (1, 1)], 1: [(2, 0)], 2: [(2, 1)], 3: [(3, 0)], 4: [(3, 1)]}
-        units = [(n, h) for n in range(N_TILES) for h in range(HALVES)]
+        round_weights(1, 1)
+        quantize_weights(1, 1)
+        clear_window(2)
+        later = [(2, 0), (2, 1), (3, 0), (3, 1)]
+        units = [(0, 0), (1, 0), (0, 1), (1, 1)] + later
         for u, (n, h) in enumerate(units):
             gate = turn_gate(weighted)
             message = messages(n, h)
             if u + 1 < len(units):
-                weighted = weighted_gate(*units[u + 1])
-            for key in rounded_at.get(u, []):
-                round_weights(*key)
-            for key in quantized_at.get(u, []):
-                quantize_weights(*key)
+                weighted = weighted_gate(u + 1, *units[u + 1])
+            if 1 <= u <= len(later):
+                round_weights(*later[u - 1])
+            if 2 <= u <= len(later) + 1:
+                quantize_weights(*later[u - 2])
             scatter(n, h, gate, message)

@@ -29,7 +29,7 @@ N_TILES = N // P
 E_TILES = HALF // P
 LIST_COLS = HALF // 16
 KIB = 1024
-EDGE = 64
+BANKS = 5
 
 
 def tile_list_rgg_relu_kernel(tc, tab_words, tab_scales, wa_words, wa_scales, wb, wc, wgo, offs, offs2, out):
@@ -38,219 +38,212 @@ def tile_list_rgg_relu_kernel(tc, tab_words, tab_scales, wa_words, wa_scales, wb
         keep = ctx.enter_context(tc.tile_pool(name="keep", bufs=1))
         ring = ctx.enter_context(tc.tile_pool(name="ring", bufs=3))
         relay = ctx.enter_context(tc.tile_pool(name="relay", bufs=1))
-        psum = ctx.enter_context(tc.psum_pool(name="psum", bufs=3))
-        turn = ctx.enter_context(tc.psum_pool(name="turn", bufs=2))
+        psum = ctx.enter_context(tc.psum_pool(name="psum", bufs=1))
 
-        def placed(name, shape, dtype, at):
-            return relay.tile(shape, dtype, name=name, offset=at, align_bytes=64)
+        def bank(name, shape, u, role):
+            return psum.tile(shape, F32, name=f"{name}{u}", offset=(3 * u + role) % BANKS * 2 * KIB)
 
-        picked_words_at = {(1, 0): 0, (0, 0): 2, (1, 1): 4, (0, 1): 6}
-        picked_scales_at = {0: 18, 1: 8}
-        parted_at = {(1, 0): 19 * KIB, (0, 0): 21 * KIB, (1, 1): 23 * KIB + EDGE, (0, 1): 27 * KIB - EDGE}
-        codes_at = {(0, 0): 0, (1, 0): 2}
-        weighted_at = {1: 29, 2: 31, 3: 33, 4: 35}
-        grouped_at = {(0, 0): 37, (0, 1): 25, (1, 0): 4, (1, 1): 39, (2, 0): 29, (2, 1): 31, (3, 0): 33, (3, 1): 35}
-        window_at = {0: 48, 1: 9, 2: 40}
+        GATE, MESSAGE = 0, 1
+        SOURCE, TARGET = 0, 1
+        weighted_at = {1: 17, 2: 20, 3: 22}
+        grouped_at = {(2, MESSAGE): 16, (2, GATE): 18, (3, MESSAGE): 20, (3, GATE): 22}
 
         lists = [keep.tile([P, J // 16], U16, name=f"list{i}") for i in range(2)]
         scale_window = keep.tile([P, T // 4], I32, align_bytes=64)
         word_window = keep.tile([P, T], I32, align_bytes=64)
         wa_codes = keep.tile([P, PASSES, N], I32, align_bytes=64)
         wa_plane = keep.tile([P, PASSES, N // 4], I32, align_bytes=64)
-        shifted_scales = [keep.tile([P, 2, HALF // 4], I32, name=f"shifted_scales{h}", align_bytes=64) for h in range(HALVES)]
-        out_windows = {}
+        picked_scales = [keep.tile([P, J], U8, name=f"picked_scales{i}", align_bytes=64) for i in range(2)]
+        shifted_scales = [keep.tile([P, J // 4], I32, name=f"shifted_scales{i}", align_bytes=64) for i in range(2)]
+        out_windows = [keep.tile([P, T], F32, name=f"out_window{i}", align_bytes=64) for i in range(2)]
         weight_rows = keep.tile([P, P], F32, align_bytes=64)
         edge_weight = keep.tile([P, J // P], F32)
         identity = keep.tile([P, P], F32, align_bytes=64)
-        planes = keep.tile([P, N_TILES, 2, PASSES, P], U8, align_bytes=64)
         warm = keep.tile([P, 8], F32)
-
-        def clear_window(i):
-            out_windows[i] = placed(f"out_window{i}", [P, T], F32, window_at[i] * KIB)
-            nc.gpsimd.memset(out_windows[i][:], 0.0)
 
         nc.gpsimd.memset(scale_window[:], 0)
         nc.gpsimd.memset(warm[:], 0.0)
         nc.scalar.activation(out=warm[:, 0:1], in_=warm[:, 1:2], func=SIGMOID)
-        nc.gpsimd.memset(shifted_scales[0][:], 0)
-        clear_window(0)
         nc.gpsimd.memset(weight_rows[:], 0.0)
-        nc.gpsimd.memset(wa_plane[:], 0)
-        nc.gpsimd.dma_start(out=weight_rows[0 : J // P, :], in_=wgo[0].rearrange("(c p) -> c p", p=P))
         make_identity(nc, identity[:])
-        nc.gpsimd.memset(shifted_scales[1][:], 0)
-
-        raw = {}
-
-        def load_weight(w, first, last):
-            for a in range(PASSES):
-                t = keep.tile([P, PACK, (last - first) * P], F32, name=f"raw{first}_{w}_{a}")
-                nc.sync.dma_start(
-                    out=t[:],
-                    in_=(wb, wc)[w][a * K_PASS : (a + 1) * K_PASS, first * P : last * P].rearrange("(p i) n -> p i n", i=PACK),
-                )
-                for n in range(first, last):
-                    raw[n, w, a] = t[:, :, (n - first) * P : (n - first + 1) * P]
-
-        nc.sync.dma_start(lists[1][:], offs2)
-        nc.sync.dma_start(lists[0][:], offs)
-        for q in range(4):
-            nc.sync.dma_start(
-                out=scale_window[32 * q : 32 * q + 8, :],
-                in_=tab_scales[:, 4 * q : 4 * q + 4, :].bitcast(I32),
-            )
-        nc.sync.dma_start(out=word_window[:], in_=tab_words[0].rearrange("p t b -> p (t b)").bitcast(I32))
-        load_weight(0, 0, 2)
-        nc.sync.dma_start(out=wa_codes[:], in_=wa_words.rearrange("a p n i -> p a (n i)").bitcast(I32))
+        for i in (SOURCE, TARGET):
+            nc.gpsimd.memset(shifted_scales[i][:], 0)
+        nc.gpsimd.memset(out_windows[0][:], 0.0)
+        nc.gpsimd.memset(wa_plane[:], 0)
+        nc.gpsimd.memset(out_windows[1][:], 0.0)
         for q in range(4):
             nc.scalar.dma_start(
                 out=wa_plane[32 * q : 32 * q + 4, :, :],
                 in_=wa_scales[:, 4 * q : 4 * q + 4, :].bitcast(I32).rearrange("a r c -> r a c"),
             )
-        load_weight(1, 0, 2)
-        load_weight(0, 2, 4)
-        load_weight(1, 2, 4)
+        nc.scalar.dma_start(out=weight_rows[0 : J // P, :], in_=wgo[0].rearrange("(c p) -> c p", p=P))
 
-        turned_rows = turn.tile([P, HALF], F32, name="turned")
+        raw = {}
+
+        def load_weight(w, pair):
+            if (w, pair) == (MESSAGE, 1):
+                raw[w, pair] = relay.tile([P, PASSES, PACK, 2 * P], F32, name="raw_held", offset=8 * KIB, align_bytes=64)
+            else:
+                raw[w, pair] = keep.tile([P, PASSES, PACK, 2 * P], F32, name=f"raw{w}_{pair}")
+            for a in range(PASSES):
+                nc.sync.dma_start(
+                    out=raw[w, pair][:, a],
+                    in_=(wb, wc)[w][a * K_PASS : (a + 1) * K_PASS, 2 * P * pair : 2 * P * (pair + 1)].rearrange("(p i) n -> p i n", i=PACK),
+                )
+
+        nc.sync.dma_start(lists[SOURCE][:], offs)
+        nc.sync.dma_start(lists[TARGET][:], offs2)
+        scale_rows = tab_scales.bitcast(I32).rearrange("a (q r) c -> r q a c", r=4)
+        for r in range(4):
+            nc.sync.dma_start(out=scale_window[r:P:16, :], in_=scale_rows[r])
+        nc.sync.dma_start(out=word_window[:], in_=tab_words[0].rearrange("p t b -> p (t b)").bitcast(I32))
+        load_weight(MESSAGE, 0)
+        load_weight(GATE, 0)
+        nc.sync.dma_start(out=wa_codes[:], in_=wa_words.rearrange("a p n i -> p a (n i)").bitcast(I32))
+
+        turned_rows = psum.tile([P, HALF], F32, name="turned_rows", offset=BANKS * 2 * KIB)
         nc.tensor.transpose(turned_rows[:, 0:P], weight_rows[:], identity[:])
         nc.scalar.copy(out=edge_weight[:], in_=turned_rows[:, 0 : J // P])
 
-        grouped = {}
         codes = {}
-        picked_scales = {}
+        planes = {}
         picked_words = {}
         parted = {}
 
-        def round_weights(n, w):
-            width = PASSES * K_PASS * (3 if (n, w) == (1, 0) else 1)
-            flat = placed(f"grouped{n}_{w}", [P, width], BF16, grouped_at[n, w] * KIB)[:, 0 : PASSES * K_PASS]
-            grouped[n, w] = flat
+        def quantize(w, tiles, rounded):
+            width = len(tiles) * PASSES * P
+            words = keep.tile([P, width], U32, name=f"codes{w}_{tiles[0]}", align_bytes=64)
+            plane = keep.tile([P, width], U8, name=f"plane{w}_{tiles[0]}", align_bytes=64)
+            nc.vector.quantize_mx(out=words[:].bitcast(FP8X4), scales=plane[:], in_=rounded)
+            for k, n in enumerate(tiles):
+                for a in range(PASSES):
+                    cols = slice((k * PASSES + a) * P, (k * PASSES + a + 1) * P)
+                    codes[w, n, a] = words[:, cols].bitcast(FP8X4)
+                    planes[w, n, a] = plane[:, cols]
+
+        def round_first_pair(w):
+            if w == GATE:
+                flat = relay.tile([P, 2, PASSES, K_PASS], BF16, name="grouped_first", offset=0, align_bytes=64)
+            else:
+                flat = keep.tile([P, 2, PASSES, K_PASS], BF16, name="grouped_pair", align_bytes=64)
             for a in range(PASSES):
                 nc.scalar.copy(
-                    out=flat[:, a * K_PASS : (a + 1) * K_PASS].rearrange("p (c m i) -> p c i m", m=4, i=PACK),
-                    in_=raw[n, w, a].rearrange("p i (c m) -> p c i m", m=4),
+                    out=flat[:, :, a, :].rearrange("p n (c m i) -> p n c i m", m=4, i=PACK),
+                    in_=raw[w, 0][:, a].rearrange("p i (n c m) -> p n c i m", n=2, m=4),
                 )
+            quantize(w, (0, 1), flat[:].rearrange("p n a c -> p (n a c)"))
 
-        def quantize_weights(n, w):
-            if (n, w) in codes_at:
-                codes[n, w] = placed(f"codes{n}_{w}", [P, PASSES, P], U32, codes_at[n, w] * KIB)
-            else:
-                codes[n, w] = keep.tile([P, PASSES, P], U32, name=f"codes{n}_{w}", align_bytes=64)
-            nc.vector.quantize_mx(
-                out=codes[n, w][:].rearrange("p a n -> p (a n)").bitcast(FP8X4),
-                scales=planes[:, n, w].rearrange("p a n -> p (a n)"),
-                in_=grouped[n, w],
+        def round_tile(n, w):
+            flat = relay.tile([P, PASSES, K_PASS], BF16, name=f"grouped{n}_{w}", offset=grouped_at[n, w] * KIB, align_bytes=64)
+            nc.scalar.copy(
+                out=flat[:].rearrange("p a (c m i) -> p a c i m", m=4, i=PACK),
+                in_=raw[w, 1][:, :, :, (n - 2) * P : (n - 1) * P].rearrange("p a i (c m) -> p a c i m", m=4),
             )
+            quantize(w, (n,), flat[:].rearrange("p a c -> p (a c)"))
 
         def list_half(i, h):
             return lists[i][:, h * LIST_COLS : (h + 1) * LIST_COLS]
 
-        def pick_scales(h, queue):
-            picked_scales[h] = placed(f"picked_scales{h}", [P, 2, HALF], U8, picked_scales_at[h] * KIB)
-            for i in (1, 0):
-                nc.vector.tensor_copy(out=picked_scales[h][:, i, :], in_=scale_window[:].bitcast(U8).indirect(list_half(i, h)))
-            queue.dma_start(out=shifted_scales[h][0:100], in_=picked_scales[h][4:104].bitcast(I32))
+        def pick_scales(i, queue):
+            nc.vector.tensor_copy(out=picked_scales[i][:], in_=scale_window[:].bitcast(U8).indirect(lists[i][:]))
+            queue.dma_start(out=shifted_scales[i][0:100], in_=picked_scales[i][16:116].bitcast(I32))
 
-        def pick_words(i, h):
-            picked_words[i, h] = placed(f"picked_words{i}_{h}", [P, HALF], U32, picked_words_at[i, h] * KIB)
-            nc.vector.tensor_copy(out=picked_words[i, h][:], in_=word_window[:].bitcast(U32).indirect(list_half(i, h)))
+        def pick_words(h):
+            if h == 0:
+                picked_words[h] = relay.tile([P, 2, HALF], U32, name="picked_words0", offset=8 * KIB, align_bytes=64)
+            else:
+                picked_words[h] = relay.tile([P, 2, HALF], U32, name="picked_words1", offset=0, align_bytes=64)
+            for i in (SOURCE, TARGET):
+                nc.vector.tensor_copy(out=picked_words[h][:, i, :], in_=word_window[:].bitcast(U32).indirect(list_half(i, h)))
 
         def part_words(i, h):
-            parted[i, h] = placed(f"parted{i}_{h}", [P, PASSES, 2 * HALF], U8, parted_at[i, h])
+            parted[i, h] = keep.tile([P, PASSES, 2 * HALF], U8, name=f"parted{i}_{h}", align_bytes=64)
             nc.vector.tensor_copy(
                 out=parted[i, h][:].bitcast(U16),
-                in_=picked_words[i, h][:].bitcast(U16).rearrange("p (j d) -> p d j", d=PASSES),
+                in_=picked_words[h][:, i, :].bitcast(U16).rearrange("p (j d) -> p d j", d=PASSES),
             )
 
         def table_operand(i, h, a, first, width):
-            cols = slice(first, first + width)
-            plane = picked_scales[h][:, i, cols] if a == 0 else shifted_scales[h][:, i, :].bitcast(U8)[:, cols]
+            cols = slice(h * HALF + first, h * HALF + first + width)
+            plane = picked_scales[i][:, cols] if a == 0 else shifted_scales[i][:].bitcast(U8)[:, cols]
             return parted[i, h][:, a, 2 * first : 2 * (first + width)].bitcast(FP4X4), plane
 
-        def weighted_gate(u, n, h):
-            cols = slice(n * P, (n + 1) * P)
-            zt = psum.tile([P, E_TILES, P], F32, name="zt")
+        def weighted_message(u, n, h):
+            mt = bank("mt", [P, E_TILES, P], u, 0)
             for e in range(E_TILES):
                 for a in range(PASSES):
-                    words, plane = table_operand(1, h, a, e * P, P)
+                    words, plane = table_operand(SOURCE, h, a, e * P, P)
                     nc.tensor.matmul_mx(
-                        out=zt[:, e, :], lhsT=words, lhsT_scale=plane,
-                        rhs=wa_codes[:, a, cols].bitcast(FP8X4), rhs_scale=wa_plane[:, a, :].bitcast(U8)[:, cols],
-                        start=(a == 0), stop=False,
+                        out=mt[:, e, :], lhsT=words, lhsT_scale=plane,
+                        rhs=codes[MESSAGE, n, a], rhs_scale=planes[MESSAGE, n, a],
+                        start=(a == 0), stop=(a == PASSES - 1),
                     )
-                    words, plane = table_operand(0, h, a, e * P, P)
-                    nc.tensor.matmul_mx(
-                        out=zt[:, e, :], lhsT=words, lhsT_scale=plane,
-                        rhs=codes[n, 0][:, a, :].bitcast(FP8X4), rhs_scale=planes[:, n, 0, a, :],
-                        start=False, stop=(a == PASSES - 1),
-                    )
-            eta = ring.tile([P, E_TILES, P], F32, name="eta")
-            nc.scalar.activation(out=eta[:], in_=zt[:], func=SIGMOID)
+            positive = ring.tile([P, E_TILES, P], F32, name="positive")
+            nc.scalar.activation(out=positive[:], in_=mt[:], func=RELU)
             if u in weighted_at:
-                weighted = placed(f"weighted{u}", [P, E_TILES, P], F32, weighted_at[u] * KIB)
+                weighted = relay.tile([P, E_TILES, P], F32, name=f"weighted{u}", offset=weighted_at[u] * KIB, align_bytes=64)
             else:
                 weighted = ring.tile([P, E_TILES, P], F32, name="weighted", align_bytes=64)
             for e in range(E_TILES):
                 c = h * E_TILES + e
-                nc.scalar.activation(out=weighted[:, e, :], in_=eta[:, e, :], func=COPY, scale=edge_weight[:, c : c + 1])
+                nc.scalar.activation(out=weighted[:, e, :], in_=positive[:, e, :], func=COPY, scale=edge_weight[:, c : c + 1])
             return weighted
 
-        def messages(n, h):
-            ms = psum.tile([P, HALF], F32, name="ms")
+        def gate_of(u, n, h):
+            cols = slice(n * P, (n + 1) * P)
+            za = bank("za", [P, HALF], u, 1)
             for a in range(PASSES):
-                words, plane = table_operand(0, h, a, 0, HALF)
+                words, plane = table_operand(SOURCE, h, a, 0, HALF)
                 nc.tensor.matmul_mx(
-                    out=ms[:], lhsT=codes[n, 1][:, a, :].bitcast(FP8X4), lhsT_scale=planes[:, n, 1, a, :],
-                    rhs=words, rhs_scale=plane, start=(a == 0), stop=(a == PASSES - 1),
+                    out=za[:], lhsT=codes[GATE, n, a], lhsT_scale=planes[GATE, n, a],
+                    rhs=words, rhs_scale=plane, start=(a == 0), stop=False,
                 )
-            message = ring.tile([P, HALF], F32, name="message")
-            nc.scalar.activation(out=message[:], in_=ms[:], func=RELU)
-            return message
+            for a in range(PASSES):
+                words, plane = table_operand(TARGET, h, a, 0, HALF)
+                nc.tensor.matmul_mx(
+                    out=za[:], lhsT=wa_codes[:, a, cols].bitcast(FP8X4), lhsT_scale=wa_plane[:, a, :].bitcast(U8)[:, cols],
+                    rhs=words, rhs_scale=plane, start=False, stop=(a == PASSES - 1),
+                )
+            gate = ring.tile([P, HALF], F32, name="gate")
+            nc.scalar.activation(out=gate[:], in_=za[:], func=SIGMOID)
+            return gate
 
-        def turn_gate(weighted):
-            turned = turn.tile([P, HALF], F32, name="turned")
+        def turn_message(u, weighted):
+            turned = bank("turned", [P, HALF], u, 2)
             for e in range(E_TILES):
                 nc.tensor.transpose(turned[:, e * P : (e + 1) * P], weighted[:, e, :], identity[:])
-            gate = ring.tile([P, HALF], F32, name="gate")
-            nc.scalar.copy(out=gate[:], in_=turned[:])
-            return gate
+            message = ring.tile([P, HALF], F32, name="message")
+            nc.scalar.copy(out=message[:], in_=turned[:])
+            return message
 
         def scatter(n, h, gate, message):
             window = out_windows[n % 3]
-            nc.vector.tensor_tensor(window[:].indirect(list_half(1, h)), message[:], gate[:], MULT)
+            nc.vector.tensor_tensor(window[:].indirect(list_half(TARGET, h)), message[:], gate[:], MULT)
             if h == HALVES - 1:
                 nc.sync.dma_start(out=out[n * P : (n + 1) * P, :], in_=window[:])
 
-        pick_scales(0, nc.scalar)
-        pick_words(1, 0)
-        pick_words(0, 0)
-        part_words(1, 0)
-        part_words(0, 0)
-        round_weights(0, 0)
-        quantize_weights(0, 0)
-        round_weights(1, 0)
-        quantize_weights(1, 0)
-        clear_window(1)
-        round_weights(0, 1)
-        weighted = weighted_gate(0, 0, 0)
-        pick_scales(1, nc.scalar)
-        pick_words(1, 1)
-        pick_words(0, 1)
-        quantize_weights(0, 1)
-        part_words(1, 1)
-        part_words(0, 1)
-        round_weights(1, 1)
-        quantize_weights(1, 1)
-        clear_window(2)
-        later = [(2, 0), (2, 1), (3, 0), (3, 1)]
-        units = [(0, 0), (1, 0), (0, 1), (1, 1)] + later
+        pick_scales(SOURCE, nc.scalar)
+        pick_scales(TARGET, nc.gpsimd)
+        pick_words(0)
+        part_words(SOURCE, 0)
+        part_words(TARGET, 0)
+        load_weight(MESSAGE, 1)
+        load_weight(GATE, 1)
+        round_first_pair(MESSAGE)
+        round_first_pair(GATE)
+        weighted = weighted_message(0, 0, 0)
+        pick_words(1)
+        part_words(SOURCE, 1)
+        part_words(TARGET, 1)
+        out_windows.append(relay.tile([P, T], F32, name="out_window2", offset=0, align_bytes=64))
+        nc.gpsimd.memset(out_windows[2][:], 0.0)
+        later = {1: [(2, MESSAGE), (2, GATE)], 2: [(3, MESSAGE)], 3: [(3, GATE)]}
+        units = [(0, 0), (1, 0), (0, 1), (1, 1), (2, 0), (2, 1), (3, 0), (3, 1)]
         for u, (n, h) in enumerate(units):
-            gate = turn_gate(weighted)
-            message = messages(n, h)
-            if u + 1 < len(units):
-                weighted = weighted_gate(u + 1, *units[u + 1])
-            if 1 <= u <= len(later):
-                round_weights(*later[u - 1])
-            if 2 <= u <= len(later) + 1:
-                quantize_weights(*later[u - 2])
+            gate = gate_of(u, n, h)
+            message = turn_message(u, weighted)
             scatter(n, h, gate, message)
+            if u + 1 < len(units):
+                weighted = weighted_message(u + 1, *units[u + 1])
+            for tile_and_weight in later.get(u, []):
+                round_tile(*tile_and_weight)

@@ -29,7 +29,7 @@ N_TILES = N // P
 E_TILES = HALF // P
 LIST_COLS = HALF // 16
 KIB = 1024
-BANKS = 5
+BANK = 2 * KIB
 
 
 def tile_list_rgg_relu_kernel(tc, tab_words, tab_scales, wa_words, wa_scales, wb, wc, wgo, offs, offs2, out):
@@ -40,13 +40,13 @@ def tile_list_rgg_relu_kernel(tc, tab_words, tab_scales, wa_words, wa_scales, wb
         relay = ctx.enter_context(tc.tile_pool(name="relay", bufs=1))
         psum = ctx.enter_context(tc.psum_pool(name="psum", bufs=1))
 
-        def bank(name, shape, u, role):
-            return psum.tile(shape, F32, name=f"{name}{u}", offset=(3 * u + role) % BANKS * 2 * KIB)
+        def bank(name, shape, index):
+            return psum.tile(shape, F32, name=name, offset=index * BANK)
 
         GATE, MESSAGE = 0, 1
         SOURCE, TARGET = 0, 1
-        weighted_at = {1: 17, 2: 20, 3: 22}
-        grouped_at = {(2, MESSAGE): 16, (2, GATE): 18, (3, MESSAGE): 20, (3, GATE): 22}
+        weighted_at = {0: 28, 1: 20, 2: 22}
+        picked_at = {(SOURCE, 0): 16, (TARGET, 0): 18, (SOURCE, 1): 24, (TARGET, 1): 6}
 
         lists = [keep.tile([P, J // 16], U16, name=f"list{i}") for i in range(2)]
         scale_window = keep.tile([P, T // 4], I32, align_bytes=64)
@@ -55,7 +55,7 @@ def tile_list_rgg_relu_kernel(tc, tab_words, tab_scales, wa_words, wa_scales, wb
         wa_plane = keep.tile([P, PASSES, N // 4], I32, align_bytes=64)
         picked_scales = [keep.tile([P, J], U8, name=f"picked_scales{i}", align_bytes=64) for i in range(2)]
         shifted_scales = [keep.tile([P, J // 4], I32, name=f"shifted_scales{i}", align_bytes=64) for i in range(2)]
-        out_windows = [keep.tile([P, T], F32, name=f"out_window{i}", align_bytes=64) for i in range(2)]
+        out_windows = {i: keep.tile([P, T], F32, name=f"out_window{i}", align_bytes=64) for i in (0, 2)}
         weight_rows = keep.tile([P, P], F32, align_bytes=64)
         edge_weight = keep.tile([P, J // P], F32)
         identity = keep.tile([P, P], F32, align_bytes=64)
@@ -68,40 +68,40 @@ def tile_list_rgg_relu_kernel(tc, tab_words, tab_scales, wa_words, wa_scales, wb
         make_identity(nc, identity[:])
         for i in (SOURCE, TARGET):
             nc.gpsimd.memset(shifted_scales[i][:], 0)
-        nc.gpsimd.memset(out_windows[0][:], 0.0)
         nc.gpsimd.memset(wa_plane[:], 0)
-        nc.gpsimd.memset(out_windows[1][:], 0.0)
-        for q in range(4):
-            nc.scalar.dma_start(
-                out=wa_plane[32 * q : 32 * q + 4, :, :],
-                in_=wa_scales[:, 4 * q : 4 * q + 4, :].bitcast(I32).rearrange("a r c -> r a c"),
-            )
+        for i in (0, 2):
+            nc.gpsimd.memset(out_windows[i][:], 0.0)
         nc.scalar.dma_start(out=weight_rows[0 : J // P, :], in_=wgo[0].rearrange("(c p) -> c p", p=P))
 
         raw = {}
 
-        def load_weight(w, pair):
-            if (w, pair) == (MESSAGE, 1):
-                raw[w, pair] = relay.tile([P, PASSES, PACK, 2 * P], F32, name="raw_held", offset=8 * KIB, align_bytes=64)
-            else:
-                raw[w, pair] = keep.tile([P, PASSES, PACK, 2 * P], F32, name=f"raw{w}_{pair}")
-            for a in range(PASSES):
-                nc.sync.dma_start(
-                    out=raw[w, pair][:, a],
-                    in_=(wb, wc)[w][a * K_PASS : (a + 1) * K_PASS, 2 * P * pair : 2 * P * (pair + 1)].rearrange("(p i) n -> p i n", i=PACK),
-                )
+        def load_pass(w, a, first, last, pool, **place):
+            t = pool.tile([P, PACK, (last - first) * P], F32, name=f"raw{w}_{a}_{first}", align_bytes=64, **place)
+            nc.sync.dma_start(
+                out=t[:],
+                in_=(wb, wc)[w][a * K_PASS : (a + 1) * K_PASS, first * P : last * P].rearrange("(p i) n -> p i n", i=PACK),
+            )
+            for n in range(first, last, 2):
+                raw[w, a, n // 2] = t[:, :, (n - first) * P : (n - first + 2) * P]
 
         nc.sync.dma_start(lists[SOURCE][:], offs)
         nc.sync.dma_start(lists[TARGET][:], offs2)
         scale_rows = tab_scales.bitcast(I32).rearrange("a (q r) c -> r q a c", r=4)
         for r in range(4):
             nc.sync.dma_start(out=scale_window[r:P:16, :], in_=scale_rows[r])
+        load_pass(MESSAGE, 0, 0, 4, keep)
         nc.sync.dma_start(out=word_window[:], in_=tab_words[0].rearrange("p t b -> p (t b)").bitcast(I32))
-        load_weight(MESSAGE, 0)
-        load_weight(GATE, 0)
+        for q in range(4):
+            nc.sync.dma_start(
+                out=wa_plane[32 * q : 32 * q + 4, :, :],
+                in_=wa_scales[:, 4 * q : 4 * q + 4, :].bitcast(I32).rearrange("a r c -> r a c"),
+            )
+        load_pass(MESSAGE, 1, 0, 2, keep)
+        load_pass(GATE, 0, 0, 2, keep)
+        load_pass(GATE, 1, 0, 2, relay, offset=32 * KIB)
         nc.sync.dma_start(out=wa_codes[:], in_=wa_words.rearrange("a p n i -> p a (n i)").bitcast(I32))
 
-        turned_rows = psum.tile([P, HALF], F32, name="turned_rows", offset=BANKS * 2 * KIB)
+        turned_rows = bank("turned_rows", [P, HALF], 0)
         nc.tensor.transpose(turned_rows[:, 0:P], weight_rows[:], identity[:])
         nc.scalar.copy(out=edge_weight[:], in_=turned_rows[:, 0 : J // P])
 
@@ -110,36 +110,23 @@ def tile_list_rgg_relu_kernel(tc, tab_words, tab_scales, wa_words, wa_scales, wb
         picked_words = {}
         parted = {}
 
-        def quantize(w, tiles, rounded):
-            width = len(tiles) * PASSES * P
-            words = keep.tile([P, width], U32, name=f"codes{w}_{tiles[0]}", align_bytes=64)
-            plane = keep.tile([P, width], U8, name=f"plane{w}_{tiles[0]}", align_bytes=64)
+        def quantize(w, parts, rounded, pool=keep, **place):
+            name = f"{w}_{parts[0][0]}_{parts[0][1]}"
+            words = pool.tile([P, len(parts) * P], U32, name=f"codes{name}", align_bytes=64, **place)
+            plane = keep.tile([P, len(parts) * P], U8, name=f"plane{name}", align_bytes=64)
             nc.vector.quantize_mx(out=words[:].bitcast(FP8X4), scales=plane[:], in_=rounded)
-            for k, n in enumerate(tiles):
-                for a in range(PASSES):
-                    cols = slice((k * PASSES + a) * P, (k * PASSES + a + 1) * P)
-                    codes[w, n, a] = words[:, cols].bitcast(FP8X4)
-                    planes[w, n, a] = plane[:, cols]
+            for k, (n, a) in enumerate(parts):
+                codes[w, n, a] = words[:, k * P : (k + 1) * P].bitcast(FP8X4)
+                planes[w, n, a] = plane[:, k * P : (k + 1) * P]
 
-        def round_first_pair(w):
-            if w == GATE:
-                flat = relay.tile([P, 2, PASSES, K_PASS], BF16, name="grouped_first", offset=0, align_bytes=64)
-            else:
-                flat = keep.tile([P, 2, PASSES, K_PASS], BF16, name="grouped_pair", align_bytes=64)
-            for a in range(PASSES):
-                nc.scalar.copy(
-                    out=flat[:, :, a, :].rearrange("p n (c m i) -> p n c i m", m=4, i=PACK),
-                    in_=raw[w, 0][:, a].rearrange("p i (n c m) -> p n c i m", n=2, m=4),
-                )
-            quantize(w, (0, 1), flat[:].rearrange("p n a c -> p (n a c)"))
-
-        def round_tile(n, w):
-            flat = relay.tile([P, PASSES, K_PASS], BF16, name=f"grouped{n}_{w}", offset=grouped_at[n, w] * KIB, align_bytes=64)
+        def round_part(dst, w, a, first, count):
             nc.scalar.copy(
-                out=flat[:].rearrange("p a (c m i) -> p a c i m", m=4, i=PACK),
-                in_=raw[w, 1][:, :, :, (n - 2) * P : (n - 1) * P].rearrange("p a i (c m) -> p a c i m", m=4),
+                out=dst.rearrange("p (n c m i) -> p n c i m", n=count, m=4, i=PACK),
+                in_=raw[w, a, first // 2][:, :, first % 2 * P : (first % 2 + count) * P].rearrange("p i (n c m) -> p n c i m", n=count, m=4),
             )
-            quantize(w, (n,), flat[:].rearrange("p a c -> p (a c)"))
+
+        def grouped_tile(name, columns, at):
+            return relay.tile([P, columns], BF16, name=name, offset=at * KIB, align_bytes=64)
 
         def list_half(i, h):
             return lists[i][:, h * LIST_COLS : (h + 1) * LIST_COLS]
@@ -148,19 +135,18 @@ def tile_list_rgg_relu_kernel(tc, tab_words, tab_scales, wa_words, wa_scales, wb
             nc.vector.tensor_copy(out=picked_scales[i][:], in_=scale_window[:].bitcast(U8).indirect(lists[i][:]))
             queue.dma_start(out=shifted_scales[i][0:100], in_=picked_scales[i][16:116].bitcast(I32))
 
-        def pick_words(h):
-            if h == 0:
-                picked_words[h] = relay.tile([P, 2, HALF], U32, name="picked_words0", offset=8 * KIB, align_bytes=64)
-            else:
-                picked_words[h] = relay.tile([P, 2, HALF], U32, name="picked_words1", offset=0, align_bytes=64)
-            for i in (SOURCE, TARGET):
-                nc.vector.tensor_copy(out=picked_words[h][:, i, :], in_=word_window[:].bitcast(U32).indirect(list_half(i, h)))
+        def pick_words(i, h):
+            picked_words[i, h] = relay.tile([P, HALF], U32, name=f"picked_words{i}_{h}", offset=picked_at[i, h] * KIB, align_bytes=64)
+            nc.vector.tensor_copy(out=picked_words[i, h][:], in_=word_window[:].bitcast(U32).indirect(list_half(i, h)))
 
         def part_words(i, h):
-            parted[i, h] = keep.tile([P, PASSES, 2 * HALF], U8, name=f"parted{i}_{h}", align_bytes=64)
+            if (i, h) == (SOURCE, 1):
+                parted[i, h] = relay.tile([P, PASSES, 2 * HALF], U8, name=f"parted{i}_{h}", offset=8 * KIB, align_bytes=64)
+            else:
+                parted[i, h] = keep.tile([P, PASSES, 2 * HALF], U8, name=f"parted{i}_{h}", align_bytes=64)
             nc.vector.tensor_copy(
                 out=parted[i, h][:].bitcast(U16),
-                in_=picked_words[h][:, i, :].bitcast(U16).rearrange("p (j d) -> p d j", d=PASSES),
+                in_=picked_words[i, h][:].bitcast(U16).rearrange("p (j d) -> p d j", d=PASSES),
             )
 
         def table_operand(i, h, a, first, width):
@@ -169,7 +155,7 @@ def tile_list_rgg_relu_kernel(tc, tab_words, tab_scales, wa_words, wa_scales, wb
             return parted[i, h][:, a, 2 * first : 2 * (first + width)].bitcast(FP4X4), plane
 
         def weighted_message(u, n, h):
-            mt = bank("mt", [P, E_TILES, P], u, 0)
+            mt = bank(f"mt{u}", [P, E_TILES, P], 4 if u == 1 else (u + 1) % 4)
             for e in range(E_TILES):
                 for a in range(PASSES):
                     words, plane = table_operand(SOURCE, h, a, e * P, P)
@@ -178,7 +164,10 @@ def tile_list_rgg_relu_kernel(tc, tab_words, tab_scales, wa_words, wa_scales, wb
                         rhs=codes[MESSAGE, n, a], rhs_scale=planes[MESSAGE, n, a],
                         start=(a == 0), stop=(a == PASSES - 1),
                     )
-            positive = ring.tile([P, E_TILES, P], F32, name="positive")
+            if u < 2:
+                positive = relay.tile([P, E_TILES, P], F32, name=f"positive{u}", offset=32 * KIB, align_bytes=64)
+            else:
+                positive = ring.tile([P, E_TILES, P], F32, name="positive")
             nc.scalar.activation(out=positive[:], in_=mt[:], func=RELU)
             if u in weighted_at:
                 weighted = relay.tile([P, E_TILES, P], F32, name=f"weighted{u}", offset=weighted_at[u] * KIB, align_bytes=64)
@@ -191,7 +180,7 @@ def tile_list_rgg_relu_kernel(tc, tab_words, tab_scales, wa_words, wa_scales, wb
 
         def gate_of(u, n, h):
             cols = slice(n * P, (n + 1) * P)
-            za = bank("za", [P, HALF], u, 1)
+            za = bank(f"za{u}", [P, HALF], 4 if u else 0)
             for a in range(PASSES):
                 words, plane = table_operand(SOURCE, h, a, 0, HALF)
                 nc.tensor.matmul_mx(
@@ -209,7 +198,7 @@ def tile_list_rgg_relu_kernel(tc, tab_words, tab_scales, wa_words, wa_scales, wb
             return gate
 
         def turn_message(u, weighted):
-            turned = bank("turned", [P, HALF], u, 2)
+            turned = bank(f"turned{u}", [P, HALF], (u + 3) % 4)
             for e in range(E_TILES):
                 nc.tensor.transpose(turned[:, e * P : (e + 1) * P], weighted[:, e, :], identity[:])
             message = ring.tile([P, HALF], F32, name="message")
@@ -224,20 +213,33 @@ def tile_list_rgg_relu_kernel(tc, tab_words, tab_scales, wa_words, wa_scales, wb
 
         pick_scales(SOURCE, nc.scalar)
         pick_scales(TARGET, nc.gpsimd)
-        pick_words(0)
+        pick_words(SOURCE, 0)
+        pick_words(TARGET, 0)
         part_words(SOURCE, 0)
         part_words(TARGET, 0)
-        load_weight(MESSAGE, 1)
-        load_weight(GATE, 1)
-        round_first_pair(MESSAGE)
-        round_first_pair(GATE)
+        load_pass(MESSAGE, 1, 2, 4, relay, offset=16 * KIB)
+        load_pass(GATE, 0, 2, 4, keep)
+        load_pass(GATE, 1, 2, 4, keep)
+        wide = 2 * K_PASS
+        first_pair = [(n, a) for a in range(PASSES) for n in (0, 1)]
+        first_message = grouped_tile("first_message", PASSES * wide, 24)
+        first_gate = grouped_tile("first_gate", PASSES * wide, 6)
+        early_message = grouped_tile("early_message", wide, 36)
+        round_part(first_message[:, 0:wide], MESSAGE, 0, 0, 2)
+        round_part(early_message[:], MESSAGE, 0, 2, 2)
+        round_part(first_message[:, wide : 2 * wide], MESSAGE, 1, 0, 2)
+        quantize(MESSAGE, first_pair, first_message[:])
+        for a in range(PASSES):
+            round_part(first_gate[:, a * wide : (a + 1) * wide], GATE, a, 0, 2)
+        quantize(GATE, first_pair, first_gate[:])
         weighted = weighted_message(0, 0, 0)
-        pick_words(1)
+        pick_words(SOURCE, 1)
+        pick_words(TARGET, 1)
         part_words(SOURCE, 1)
+        quantize(MESSAGE, [(2, 0), (3, 0)], early_message[:], relay, offset=24 * KIB)
         part_words(TARGET, 1)
-        out_windows.append(relay.tile([P, T], F32, name="out_window2", offset=0, align_bytes=64))
-        nc.gpsimd.memset(out_windows[2][:], 0.0)
-        later = {1: [(2, MESSAGE), (2, GATE)], 2: [(3, MESSAGE)], 3: [(3, GATE)]}
+        out_windows[1] = relay.tile([P, T], F32, name="out_window1", offset=0, align_bytes=64)
+        nc.gpsimd.memset(out_windows[1][:], 0.0)
         units = [(0, 0), (1, 0), (0, 1), (1, 1), (2, 0), (2, 1), (3, 0), (3, 1)]
         for u, (n, h) in enumerate(units):
             gate = gate_of(u, n, h)
@@ -245,5 +247,12 @@ def tile_list_rgg_relu_kernel(tc, tab_words, tab_scales, wa_words, wa_scales, wb
             scatter(n, h, gate, message)
             if u + 1 < len(units):
                 weighted = weighted_message(u + 1, *units[u + 1])
-            for tile_and_weight in later.get(u, []):
-                round_tile(*tile_and_weight)
+            if u in weighted_at:
+                late = grouped_tile(f"late{u}", wide, weighted_at[u])
+                if u == 0:
+                    round_part(late[:], MESSAGE, 1, 2, 2)
+                    quantize(MESSAGE, [(2, 1), (3, 1)], late[:])
+                else:
+                    for a in range(PASSES):
+                        round_part(late[:, a * K_PASS : (a + 1) * K_PASS], GATE, a, u + 1, 1)
+                    quantize(GATE, [(u + 1, a) for a in range(PASSES)], late[:])

@@ -45,8 +45,9 @@ def tile_list_rgg_relu_kernel(tc, tab_words, tab_scales, wa_words, wa_scales, wb
 
         GATE, MESSAGE = 0, 1
         SOURCE, TARGET = 0, 1
+        parted_at = {(TARGET, 0): 24, (SOURCE, 1): 8}
         weighted_at = {0: 28, 1: 20, 2: 22}
-        picked_at = {(SOURCE, 0): 16, (TARGET, 0): 18, (SOURCE, 1): 24, (TARGET, 1): 6}
+        picked_at = {(SOURCE, 0): 16, (TARGET, 0): 18, (SOURCE, 1): 26, (TARGET, 1): 6}
 
         lists = [keep.tile([P, J // 16], U16, name=f"list{i}") for i in range(2)]
         scale_window = keep.tile([P, T // 4], I32, align_bytes=64)
@@ -140,8 +141,8 @@ def tile_list_rgg_relu_kernel(tc, tab_words, tab_scales, wa_words, wa_scales, wb
             nc.vector.tensor_copy(out=picked_words[i, h][:], in_=word_window[:].bitcast(U32).indirect(list_half(i, h)))
 
         def part_words(i, h):
-            if (i, h) == (SOURCE, 1):
-                parted[i, h] = relay.tile([P, PASSES, 2 * HALF], U8, name=f"parted{i}_{h}", offset=8 * KIB, align_bytes=64)
+            if (i, h) in parted_at:
+                parted[i, h] = relay.tile([P, PASSES, 2 * HALF], U8, name=f"parted{i}_{h}", offset=parted_at[i, h] * KIB, align_bytes=64)
             else:
                 parted[i, h] = keep.tile([P, PASSES, 2 * HALF], U8, name=f"parted{i}_{h}", align_bytes=64)
             nc.vector.tensor_copy(
@@ -216,10 +217,6 @@ def tile_list_rgg_relu_kernel(tc, tab_words, tab_scales, wa_words, wa_scales, wb
         pick_words(SOURCE, 0)
         pick_words(TARGET, 0)
         part_words(SOURCE, 0)
-        part_words(TARGET, 0)
-        load_pass(MESSAGE, 1, 2, 4, relay, offset=16 * KIB)
-        load_pass(GATE, 0, 2, 4, keep)
-        load_pass(GATE, 1, 2, 4, keep)
         wide = 2 * K_PASS
         first_pair = [(n, a) for a in range(PASSES) for n in (0, 1)]
         first_message = grouped_tile("first_message", PASSES * wide, 24)
@@ -229,6 +226,10 @@ def tile_list_rgg_relu_kernel(tc, tab_words, tab_scales, wa_words, wa_scales, wb
         round_part(early_message[:], MESSAGE, 0, 2, 2)
         round_part(first_message[:, wide : 2 * wide], MESSAGE, 1, 0, 2)
         quantize(MESSAGE, first_pair, first_message[:])
+        part_words(TARGET, 0)
+        load_pass(MESSAGE, 1, 2, 4, relay, offset=16 * KIB)
+        load_pass(GATE, 0, 2, 4, keep)
+        load_pass(GATE, 1, 2, 4, keep)
         for a in range(PASSES):
             round_part(first_gate[:, a * wide : (a + 1) * wide], GATE, a, 0, 2)
         quantize(GATE, first_pair, first_gate[:])
@@ -236,11 +237,11 @@ def tile_list_rgg_relu_kernel(tc, tab_words, tab_scales, wa_words, wa_scales, wb
         pick_words(SOURCE, 1)
         pick_words(TARGET, 1)
         part_words(SOURCE, 1)
-        quantize(MESSAGE, [(2, 0), (3, 0)], early_message[:], relay, offset=24 * KIB)
+        quantize(MESSAGE, [(2, 0), (3, 0)], early_message[:], relay, offset=26 * KIB)
         part_words(TARGET, 1)
         out_windows[1] = relay.tile([P, T], F32, name="out_window1", offset=0, align_bytes=64)
         nc.gpsimd.memset(out_windows[1][:], 0.0)
-        units = [(0, 0), (1, 0), (0, 1), (1, 1), (2, 0), (2, 1), (3, 0), (3, 1)]
+        units = [(0, 0), (1, 0), (0, 1), (1, 1), (2, 0), (3, 0), (2, 1), (3, 1)]
         for u, (n, h) in enumerate(units):
             gate = gate_of(u, n, h)
             message = turn_message(u, weighted)

@@ -56,7 +56,7 @@ def tile_list_rgg_relu_kernel(tc, tab_words, tab_scales, wa_words, wa_scales, wb
         wa_plane = keep.tile([P, PASSES, N // 4], I32, align_bytes=64)
         picked_scales = [keep.tile([P, J], U8, name=f"picked_scales{i}", align_bytes=64) for i in range(2)]
         shifted_scales = [keep.tile([P, J // 4], I32, name=f"shifted_scales{i}", align_bytes=64) for i in range(2)]
-        out_windows = {i: keep.tile([P, T], F32, name=f"out_window{i}", align_bytes=64) for i in (0, 2)}
+        out_windows = {i: keep.tile([P, T], F32, name=f"out_window{i}", align_bytes=64) for i in (0,)}
         weight_rows = keep.tile([P, P], F32, align_bytes=64)
         edge_weight = keep.tile([P, J // P], F32)
         identity = keep.tile([P, P], F32, align_bytes=64)
@@ -70,8 +70,7 @@ def tile_list_rgg_relu_kernel(tc, tab_words, tab_scales, wa_words, wa_scales, wb
         for i in (SOURCE, TARGET):
             nc.gpsimd.memset(shifted_scales[i][:], 0)
         nc.gpsimd.memset(wa_plane[:], 0)
-        for i in (0, 2):
-            nc.gpsimd.memset(out_windows[i][:], 0.0)
+        nc.gpsimd.memset(out_windows[0][:], 0.0)
         nc.scalar.dma_start(out=weight_rows[0 : J // P, :], in_=wgo[0].rearrange("(c p) -> c p", p=P))
 
         raw = {}
@@ -253,6 +252,8 @@ def tile_list_rgg_relu_kernel(tc, tab_words, tab_scales, wa_words, wa_scales, wb
                 if u == 0:
                     round_part(late[:], MESSAGE, 1, 2, 2)
                     quantize(MESSAGE, [(2, 1), (3, 1)], late[:])
+                    out_windows[2] = relay.tile([P, T], F32, name="out_window2", offset=28 * KIB, align_bytes=64)
+                    nc.gpsimd.memset(out_windows[2][:], 0.0)
                 else:
                     for a in range(PASSES):
                         round_part(late[:, a * K_PASS : (a + 1) * K_PASS], GATE, a, u + 1, 1)

@@ -25,11 +25,12 @@ PASSES = 2
 K_PASS = P * PACK
 HALF = 512
 HALVES = J // HALF
-N_TILES = N // P
 E_TILES = HALF // P
 LIST_COLS = HALF // 16
 KIB = 1024
 BANK = 2 * KIB
+SHIFT = 16
+PLANE_ROWS = 100
 
 
 def tile_list_rgg_relu_kernel(tc, tab_words, tab_scales, wa_words, wa_scales, wb, wc, wgo, offs, offs2, out):
@@ -43,20 +44,21 @@ def tile_list_rgg_relu_kernel(tc, tab_words, tab_scales, wa_words, wa_scales, wb
         def bank(name, shape, index):
             return psum.tile(shape, F32, name=name, offset=index * BANK)
 
+        def placed(name, shape, dtype, at):
+            if at is None:
+                return keep.tile(shape, dtype, name=name, align_bytes=64)
+            return relay.tile(shape, dtype, name=name, offset=at * KIB, align_bytes=64)
+
         GATE, MESSAGE = 0, 1
         SOURCE, TARGET = 0, 1
-        parted_at = {(TARGET, 0): 24, (SOURCE, 1): 8}
-        weighted_at = {0: 28, 1: 20, 2: 22}
-        picked_at = {(SOURCE, 0): 16, (TARGET, 0): 18, (SOURCE, 1): 26, (TARGET, 1): 6}
 
         lists = [keep.tile([P, J // 16], U16, name=f"list{i}") for i in range(2)]
         scale_window = keep.tile([P, T // 4], I32, align_bytes=64)
         word_window = keep.tile([P, T], I32, align_bytes=64)
         wa_codes = keep.tile([P, PASSES, N], I32, align_bytes=64)
         wa_plane = keep.tile([P, PASSES, N // 4], I32, align_bytes=64)
-        picked_scales = [keep.tile([P, J], U8, name=f"picked_scales{i}", align_bytes=64) for i in range(2)]
-        shifted_scales = [keep.tile([P, J // 4], I32, name=f"shifted_scales{i}", align_bytes=64) for i in range(2)]
-        out_windows = {i: keep.tile([P, T], F32, name=f"out_window{i}", align_bytes=64) for i in (0,)}
+        shifted = [keep.tile([P, c * HALF // 4], I32, name=f"shifted{c}", align_bytes=64) for c in (3, 1)]
+        out_windows = {0: keep.tile([P, T], F32, name="out_window0", align_bytes=64)}
         weight_rows = keep.tile([P, P], F32, align_bytes=64)
         edge_weight = keep.tile([P, J // P], F32)
         identity = keep.tile([P, P], F32, align_bytes=64)
@@ -66,53 +68,51 @@ def tile_list_rgg_relu_kernel(tc, tab_words, tab_scales, wa_words, wa_scales, wb
         nc.gpsimd.memset(warm[:], 0.0)
         nc.scalar.activation(out=warm[:, 0:1], in_=warm[:, 1:2], func=SIGMOID)
         nc.gpsimd.memset(weight_rows[:], 0.0)
-        make_identity(nc, identity[:])
-        for i in (SOURCE, TARGET):
-            nc.gpsimd.memset(shifted_scales[i][:], 0)
         nc.gpsimd.memset(wa_plane[:], 0)
+        make_identity(nc, identity[:])
+        for tile in shifted:
+            nc.gpsimd.memset(tile[:], 0)
         nc.gpsimd.memset(out_windows[0][:], 0.0)
-        nc.scalar.dma_start(out=weight_rows[0 : J // P, :], in_=wgo[0].rearrange("(c p) -> c p", p=P))
 
         raw = {}
 
-        def load_pass(w, a, first, last, pool, **place):
-            t = pool.tile([P, PACK, (last - first) * P], F32, name=f"raw{w}_{a}_{first}", align_bytes=64, **place)
+        def load_pair(w, a, pair, at=None):
+            t = placed(f"raw{w}_{a}_{pair}", [P, PACK, 2 * P], F32, at)
             nc.sync.dma_start(
                 out=t[:],
-                in_=(wb, wc)[w][a * K_PASS : (a + 1) * K_PASS, first * P : last * P].rearrange("(p i) n -> p i n", i=PACK),
+                in_=(wb, wc)[w][a * K_PASS : (a + 1) * K_PASS, pair * 2 * P : (pair + 1) * 2 * P].rearrange("(p i) n -> p i n", i=PACK),
             )
-            for n in range(first, last, 2):
-                raw[w, a, n // 2] = t[:, :, (n - first) * P : (n - first + 2) * P]
+            raw[w, a, pair] = t
 
-        nc.sync.dma_start(lists[SOURCE][:], offs)
         nc.sync.dma_start(lists[TARGET][:], offs2)
+        nc.sync.dma_start(lists[SOURCE][:], offs)
         scale_rows = tab_scales.bitcast(I32).rearrange("a (q r) c -> r q a c", r=4)
         for r in range(4):
-            nc.sync.dma_start(out=scale_window[r:P:16, :], in_=scale_rows[r])
-        load_pass(MESSAGE, 0, 0, 4, keep)
+            nc.sync.dma_start(out=scale_window[r:P:SHIFT, :], in_=scale_rows[r])
+        load_pair(MESSAGE, 0, 0)
         nc.sync.dma_start(out=word_window[:], in_=tab_words[0].rearrange("p t b -> p (t b)").bitcast(I32))
+        nc.sync.dma_start(out=weight_rows[0 : J // P, :], in_=wgo[0].rearrange("(c p) -> c p", p=P))
         for q in range(4):
             nc.sync.dma_start(
                 out=wa_plane[32 * q : 32 * q + 4, :, :],
                 in_=wa_scales[:, 4 * q : 4 * q + 4, :].bitcast(I32).rearrange("a r c -> r a c"),
             )
-        load_pass(MESSAGE, 1, 0, 2, keep)
-        load_pass(GATE, 0, 0, 2, keep)
-        load_pass(GATE, 1, 0, 2, relay, offset=32 * KIB)
-        nc.sync.dma_start(out=wa_codes[:], in_=wa_words.rearrange("a p n i -> p a (n i)").bitcast(I32))
+        load_pair(MESSAGE, 1, 0)
+        load_pair(GATE, 0, 0)
+        load_pair(GATE, 1, 0)
 
-        turned_rows = bank("turned_rows", [P, HALF], 0)
+        turned_rows = bank("turned_rows", [P, HALF], 6)
         nc.tensor.transpose(turned_rows[:, 0:P], weight_rows[:], identity[:])
-        nc.scalar.copy(out=edge_weight[:], in_=turned_rows[:, 0 : J // P])
 
         codes = {}
         planes = {}
+        picked_scales = {}
         picked_words = {}
         parted = {}
 
-        def quantize(w, parts, rounded, pool=keep, **place):
+        def quantize(w, parts, rounded):
             name = f"{w}_{parts[0][0]}_{parts[0][1]}"
-            words = pool.tile([P, len(parts) * P], U32, name=f"codes{name}", align_bytes=64, **place)
+            words = keep.tile([P, len(parts) * P], U32, name=f"codes{name}", align_bytes=64)
             plane = keep.tile([P, len(parts) * P], U8, name=f"plane{name}", align_bytes=64)
             nc.vector.quantize_mx(out=words[:].bitcast(FP8X4), scales=plane[:], in_=rounded)
             for k, (n, a) in enumerate(parts):
@@ -125,37 +125,36 @@ def tile_list_rgg_relu_kernel(tc, tab_words, tab_scales, wa_words, wa_scales, wb
                 in_=raw[w, a, first // 2][:, :, first % 2 * P : (first % 2 + count) * P].rearrange("p i (n c m) -> p n c i m", n=count, m=4),
             )
 
-        def grouped_tile(name, columns, at):
-            return relay.tile([P, columns], BF16, name=name, offset=at * KIB, align_bytes=64)
+        def list_halves(i, h, count=1):
+            return lists[i][:, h * LIST_COLS : (h + count) * LIST_COLS]
 
-        def list_half(i, h):
-            return lists[i][:, h * LIST_COLS : (h + 1) * LIST_COLS]
+        def pick_scales(runs, moved, queue, at=None):
+            picked = placed(f"picked_scales{len(runs)}", [P, sum(count for i, h, count in runs) * HALF], U8, at)
+            first = 0
+            for i, h, count in runs:
+                nc.vector.tensor_copy(out=picked[:, first * HALF : (first + count) * HALF], in_=scale_window[:].bitcast(U8).indirect(list_halves(i, h, count)))
+                for k in range(count):
+                    cols = slice((first + k) * HALF, (first + k + 1) * HALF)
+                    picked_scales[i, h + k] = (picked[:, cols], moved[:].bitcast(U8)[:, cols])
+                first = first + count
+            queue.dma_start(out=moved[0:PLANE_ROWS], in_=picked[SHIFT : SHIFT + PLANE_ROWS].bitcast(I32))
 
-        def pick_scales(i, queue):
-            nc.vector.tensor_copy(out=picked_scales[i][:], in_=scale_window[:].bitcast(U8).indirect(lists[i][:]))
-            queue.dma_start(out=shifted_scales[i][0:100], in_=picked_scales[i][16:116].bitcast(I32))
-
-        def pick_words(i, h):
-            picked_words[i, h] = relay.tile([P, HALF], U32, name=f"picked_words{i}_{h}", offset=picked_at[i, h] * KIB, align_bytes=64)
-            nc.vector.tensor_copy(out=picked_words[i, h][:], in_=word_window[:].bitcast(U32).indirect(list_half(i, h)))
+        def pick_words(i, h, at=None):
+            picked_words[i, h] = placed(f"picked_words{i}_{h}", [P, HALF], U32, at)
+            nc.vector.tensor_copy(out=picked_words[i, h][:], in_=word_window[:].bitcast(U32).indirect(list_halves(i, h)))
 
         def part_words(i, h):
-            if (i, h) in parted_at:
-                parted[i, h] = relay.tile([P, PASSES, 2 * HALF], U8, name=f"parted{i}_{h}", offset=parted_at[i, h] * KIB, align_bytes=64)
-            else:
-                parted[i, h] = keep.tile([P, PASSES, 2 * HALF], U8, name=f"parted{i}_{h}", align_bytes=64)
+            parted[i, h] = keep.tile([P, PASSES, 2 * HALF], U8, name=f"parted{i}_{h}", align_bytes=64)
             nc.vector.tensor_copy(
                 out=parted[i, h][:].bitcast(U16),
                 in_=picked_words[i, h][:].bitcast(U16).rearrange("p (j d) -> p d j", d=PASSES),
             )
 
         def table_operand(i, h, a, first, width):
-            cols = slice(h * HALF + first, h * HALF + first + width)
-            plane = picked_scales[i][:, cols] if a == 0 else shifted_scales[i][:].bitcast(U8)[:, cols]
-            return parted[i, h][:, a, 2 * first : 2 * (first + width)].bitcast(FP4X4), plane
+            return parted[i, h][:, a, 2 * first : 2 * (first + width)].bitcast(FP4X4), picked_scales[i, h][a][:, first : first + width]
 
-        def weighted_message(u, n, h):
-            mt = bank(f"mt{u}", [P, E_TILES, P], 4 if u == 1 else (u + 1) % 4)
+        def weighted_message(u, n, h, positive_at=None, weighted_at=None):
+            mt = bank(f"mt{u}", [P, E_TILES, P], 4 if u < 2 else (u + 1) % 4)
             for e in range(E_TILES):
                 for a in range(PASSES):
                     words, plane = table_operand(SOURCE, h, a, e * P, P)
@@ -164,33 +163,36 @@ def tile_list_rgg_relu_kernel(tc, tab_words, tab_scales, wa_words, wa_scales, wb
                         rhs=codes[MESSAGE, n, a], rhs_scale=planes[MESSAGE, n, a],
                         start=(a == 0), stop=(a == PASSES - 1),
                     )
-            if u < 2:
-                positive = relay.tile([P, E_TILES, P], F32, name=f"positive{u}", offset=32 * KIB, align_bytes=64)
-            else:
+            if positive_at is None:
                 positive = ring.tile([P, E_TILES, P], F32, name="positive")
-            nc.scalar.activation(out=positive[:], in_=mt[:], func=RELU)
-            if u in weighted_at:
-                weighted = relay.tile([P, E_TILES, P], F32, name=f"weighted{u}", offset=weighted_at[u] * KIB, align_bytes=64)
             else:
+                positive = placed(f"positive{u}", [P, E_TILES, P], F32, positive_at)
+            nc.scalar.activation(out=positive[:], in_=mt[:], func=RELU)
+            if weighted_at is None:
                 weighted = ring.tile([P, E_TILES, P], F32, name="weighted", align_bytes=64)
+            else:
+                weighted = placed(f"weighted{u}", [P, E_TILES, P], F32, weighted_at)
             for e in range(E_TILES):
                 c = h * E_TILES + e
                 nc.scalar.activation(out=weighted[:, e, :], in_=positive[:, e, :], func=COPY, scale=edge_weight[:, c : c + 1])
             return weighted
 
-        def gate_of(u, n, h):
+        def open_gate(u, n, h):
             cols = slice(n * P, (n + 1) * P)
-            za = bank(f"za{u}", [P, HALF], 4 if u else 0)
-            for a in range(PASSES):
-                words, plane = table_operand(SOURCE, h, a, 0, HALF)
-                nc.tensor.matmul_mx(
-                    out=za[:], lhsT=codes[GATE, n, a], lhsT_scale=planes[GATE, n, a],
-                    rhs=words, rhs_scale=plane, start=(a == 0), stop=False,
-                )
+            za = bank(f"za{u}", [P, HALF], 5)
             for a in range(PASSES):
                 words, plane = table_operand(TARGET, h, a, 0, HALF)
                 nc.tensor.matmul_mx(
                     out=za[:], lhsT=wa_codes[:, a, cols].bitcast(FP8X4), lhsT_scale=wa_plane[:, a, :].bitcast(U8)[:, cols],
+                    rhs=words, rhs_scale=plane, start=(a == 0), stop=False,
+                )
+            return za
+
+        def close_gate(za, n, h):
+            for a in range(PASSES):
+                words, plane = table_operand(SOURCE, h, a, 0, HALF)
+                nc.tensor.matmul_mx(
+                    out=za[:], lhsT=codes[GATE, n, a], lhsT_scale=planes[GATE, n, a],
                     rhs=words, rhs_scale=plane, start=False, stop=(a == PASSES - 1),
                 )
             gate = ring.tile([P, HALF], F32, name="gate")
@@ -207,54 +209,60 @@ def tile_list_rgg_relu_kernel(tc, tab_words, tab_scales, wa_words, wa_scales, wb
 
         def scatter(n, h, gate, message):
             window = out_windows[n % 3]
-            nc.vector.tensor_tensor(window[:].indirect(list_half(TARGET, h)), message[:], gate[:], MULT)
+            nc.vector.tensor_tensor(window[:].indirect(list_halves(TARGET, h)), message[:], gate[:], MULT)
             if h == HALVES - 1:
                 nc.sync.dma_start(out=out[n * P : (n + 1) * P, :], in_=window[:])
 
-        pick_scales(SOURCE, nc.scalar)
-        pick_scales(TARGET, nc.gpsimd)
-        pick_words(SOURCE, 0)
-        pick_words(TARGET, 0)
-        part_words(SOURCE, 0)
         wide = 2 * K_PASS
         first_pair = [(n, a) for a in range(PASSES) for n in (0, 1)]
-        first_message = grouped_tile("first_message", PASSES * wide, 24)
-        first_gate = grouped_tile("first_gate", PASSES * wide, 6)
-        early_message = grouped_tile("early_message", wide, 36)
-        round_part(first_message[:, 0:wide], MESSAGE, 0, 0, 2)
-        round_part(early_message[:], MESSAGE, 0, 2, 2)
-        round_part(first_message[:, wide : 2 * wide], MESSAGE, 1, 0, 2)
-        quantize(MESSAGE, first_pair, first_message[:])
+        late_parts = {1: (MESSAGE, [(2, 1), (3, 1)]), 2: (GATE, [(2, 0), (2, 1)]), 3: (GATE, [(3, 0), (3, 1)])}
+        units = [(0, 0), (1, 0), (0, 1), (1, 1), (2, 0), (3, 0), (2, 1), (3, 1)]
+        weighted_at = {1: 28, 2: 38, 3: 40}
+
+        pick_scales([(TARGET, 0, 2), (SOURCE, 0, 1)], shifted[0], nc.sync)
+        load_pair(MESSAGE, 0, 1, 12)
+        nc.sync.dma_start(out=wa_codes[:], in_=wa_words.rearrange("a p n i -> p a (n i)").bitcast(I32))
+        pick_words(TARGET, 0)
+        pick_words(SOURCE, 0)
         part_words(TARGET, 0)
-        load_pass(MESSAGE, 1, 2, 4, relay, offset=16 * KIB)
-        load_pass(GATE, 0, 2, 4, keep)
-        load_pass(GATE, 1, 2, 4, keep)
+        part_words(SOURCE, 0)
+        first_message = placed("first_message", [P, PASSES * wide], BF16, 16)
+        first_gate = placed("first_gate", [P, PASSES * wide], BF16, 6)
+        for a in range(PASSES):
+            round_part(first_message[:, a * wide : (a + 1) * wide], MESSAGE, a, 0, 2)
+        nc.scalar.copy(out=edge_weight[:], in_=turned_rows[:, 0 : J // P])
+        load_pair(MESSAGE, 1, 1)
+        load_pair(GATE, 0, 1)
+        load_pair(GATE, 1, 1)
+        quantize(MESSAGE, first_pair, first_message[:])
+        pick_scales([(SOURCE, 1, 1)], shifted[1], nc.gpsimd, 16)
         for a in range(PASSES):
             round_part(first_gate[:, a * wide : (a + 1) * wide], GATE, a, 0, 2)
         quantize(GATE, first_pair, first_gate[:])
-        weighted = weighted_message(0, 0, 0)
-        pick_words(SOURCE, 1)
-        pick_words(TARGET, 1)
+        pick_words(SOURCE, 1, 8)
+        pick_words(TARGET, 1, 6)
         part_words(SOURCE, 1)
-        quantize(MESSAGE, [(2, 0), (3, 0)], early_message[:], relay, offset=26 * KIB)
         part_words(TARGET, 1)
-        out_windows[1] = relay.tile([P, T], F32, name="out_window1", offset=0, align_bytes=64)
+        early_message = placed("early_message", [P, wide], BF16, None)
+        round_part(early_message[:], MESSAGE, 0, 2, 2)
+        quantize(MESSAGE, [(2, 0), (3, 0)], early_message[:])
+        weighted = weighted_message(0, *units[0], 12)
+        za = open_gate(0, *units[0])
+        out_windows[1] = placed("out_window1", [P, T], F32, 0)
         nc.gpsimd.memset(out_windows[1][:], 0.0)
-        units = [(0, 0), (1, 0), (0, 1), (1, 1), (2, 0), (3, 0), (2, 1), (3, 1)]
         for u, (n, h) in enumerate(units):
-            gate = gate_of(u, n, h)
+            gate = close_gate(za, n, h)
             message = turn_message(u, weighted)
             scatter(n, h, gate, message)
-            if u + 1 < len(units):
-                weighted = weighted_message(u + 1, *units[u + 1])
             if u in weighted_at:
-                late = grouped_tile(f"late{u}", wide, weighted_at[u])
-                if u == 0:
-                    round_part(late[:], MESSAGE, 1, 2, 2)
-                    quantize(MESSAGE, [(2, 1), (3, 1)], late[:])
-                    out_windows[2] = relay.tile([P, T], F32, name="out_window2", offset=28 * KIB, align_bytes=64)
+                late = placed(f"late{u}", [P, wide], BF16, weighted_at[u])
+                w, parts = late_parts[u]
+                for k, (tile_n, a) in enumerate(parts):
+                    round_part(late[:, k * K_PASS : (k + 1) * K_PASS], w, a, tile_n, 1)
+                quantize(w, parts, late[:])
+                if u == 1:
+                    out_windows[2] = placed("out_window2", [P, T], F32, 22)
                     nc.gpsimd.memset(out_windows[2][:], 0.0)
-                else:
-                    for a in range(PASSES):
-                        round_part(late[:, a * K_PASS : (a + 1) * K_PASS], GATE, a, u + 1, 1)
-                    quantize(GATE, [(u + 1, a) for a in range(PASSES)], late[:])
+            if u + 1 < len(units):
+                za = open_gate(u + 1, *units[u + 1])
+                weighted = weighted_message(u + 1, *units[u + 1], 12 if u == 0 else None, weighted_at.get(u + 1))

@@ -55,7 +55,7 @@ def tile_list_rgg_relu_kernel(tc, tab_words, tab_scales, wa_words, wa_scales, wb
         lists = [keep.tile([P, J // 16], U16, name=f"list{i}") for i in range(2)]
         scale_window = keep.tile([P, T // 4], I32, align_bytes=64)
         word_window = keep.tile([P, T], I32, align_bytes=64)
-        wa_codes = keep.tile([P, PASSES, N], I32, align_bytes=64)
+        wa_codes = [keep.tile([P, PASSES, N // 2], I32, name=f"wa_codes{pair}", align_bytes=64) for pair in range(2)]
         wa_plane = keep.tile([P, PASSES, N // 4], I32, align_bytes=64)
         shifted = [keep.tile([P, c * HALF // 4], I32, name=f"shifted{c}", align_bytes=64) for c in (3, 1)]
         out_windows = {0: keep.tile([P, T], F32, name="out_window0", align_bytes=64)}
@@ -84,13 +84,17 @@ def tile_list_rgg_relu_kernel(tc, tab_words, tab_scales, wa_words, wa_scales, wb
             )
             raw[w, a, pair] = t
 
+        def load_wa(pair):
+            words = wa_words.rearrange("a p n i -> p a (n i)").bitcast(I32)
+            nc.sync.dma_start(out=wa_codes[pair][:], in_=words[:, :, pair * 2 * P : (pair + 1) * 2 * P])
+
         nc.sync.dma_start(lists[TARGET][:], offs2)
         nc.sync.dma_start(lists[SOURCE][:], offs)
         scale_rows = tab_scales.bitcast(I32).rearrange("a (q r) c -> r q a c", r=4)
         for r in range(4):
             nc.sync.dma_start(out=scale_window[r:P:SHIFT, :], in_=scale_rows[r])
-        load_pair(MESSAGE, 0, 0)
         nc.sync.dma_start(out=word_window[:], in_=tab_words[0].rearrange("p t b -> p (t b)").bitcast(I32))
+        load_pair(MESSAGE, 0, 0)
         nc.sync.dma_start(out=weight_rows[0 : J // P, :], in_=wgo[0].rearrange("(c p) -> c p", p=P))
         for q in range(4):
             nc.sync.dma_start(
@@ -99,7 +103,7 @@ def tile_list_rgg_relu_kernel(tc, tab_words, tab_scales, wa_words, wa_scales, wb
             )
         load_pair(MESSAGE, 1, 0)
         load_pair(GATE, 0, 0)
-        load_pair(GATE, 1, 0)
+        load_pair(GATE, 1, 0, 12)
 
         turned_rows = bank("turned_rows", [P, HALF], 6)
         nc.tensor.transpose(turned_rows[:, 0:P], weight_rows[:], identity[:])
@@ -143,8 +147,8 @@ def tile_list_rgg_relu_kernel(tc, tab_words, tab_scales, wa_words, wa_scales, wb
             picked_words[i, h] = placed(f"picked_words{i}_{h}", [P, HALF], U32, at)
             nc.vector.tensor_copy(out=picked_words[i, h][:], in_=word_window[:].bitcast(U32).indirect(list_halves(i, h)))
 
-        def part_words(i, h):
-            parted[i, h] = keep.tile([P, PASSES, 2 * HALF], U8, name=f"parted{i}_{h}", align_bytes=64)
+        def part_words(i, h, at=None):
+            parted[i, h] = placed(f"parted{i}_{h}", [P, PASSES, 2 * HALF], U8, at)
             nc.vector.tensor_copy(
                 out=parted[i, h][:].bitcast(U16),
                 in_=picked_words[i, h][:].bitcast(U16).rearrange("p (j d) -> p d j", d=PASSES),
@@ -183,7 +187,7 @@ def tile_list_rgg_relu_kernel(tc, tab_words, tab_scales, wa_words, wa_scales, wb
             for a in range(PASSES):
                 words, plane = table_operand(TARGET, h, a, 0, HALF)
                 nc.tensor.matmul_mx(
-                    out=za[:], lhsT=wa_codes[:, a, cols].bitcast(FP8X4), lhsT_scale=wa_plane[:, a, :].bitcast(U8)[:, cols],
+                    out=za[:], lhsT=wa_codes[n // 2][:, a, n % 2 * P : (n % 2 + 1) * P].bitcast(FP8X4), lhsT_scale=wa_plane[:, a, :].bitcast(U8)[:, cols],
                     rhs=words, rhs_scale=plane, start=(a == 0), stop=False,
                 )
             return za
@@ -220,11 +224,10 @@ def tile_list_rgg_relu_kernel(tc, tab_words, tab_scales, wa_words, wa_scales, wb
         weighted_at = {1: 28, 2: 38, 3: 40}
 
         pick_scales([(TARGET, 0, 2), (SOURCE, 0, 1)], shifted[0], nc.sync)
-        load_pair(MESSAGE, 0, 1, 12)
-        nc.sync.dma_start(out=wa_codes[:], in_=wa_words.rearrange("a p n i -> p a (n i)").bitcast(I32))
-        pick_words(TARGET, 0)
+        load_wa(0)
+        load_pair(MESSAGE, 0, 1)
         pick_words(SOURCE, 0)
-        part_words(TARGET, 0)
+        pick_words(TARGET, 0)
         part_words(SOURCE, 0)
         first_message = placed("first_message", [P, PASSES * wide], BF16, 16)
         first_gate = placed("first_gate", [P, PASSES * wide], BF16, 6)
@@ -234,8 +237,10 @@ def tile_list_rgg_relu_kernel(tc, tab_words, tab_scales, wa_words, wa_scales, wb
         load_pair(MESSAGE, 1, 1)
         load_pair(GATE, 0, 1)
         load_pair(GATE, 1, 1)
+        load_wa(1)
         quantize(MESSAGE, first_pair, first_message[:])
-        pick_scales([(SOURCE, 1, 1)], shifted[1], nc.gpsimd, 16)
+        part_words(TARGET, 0, 16)
+        pick_scales([(SOURCE, 1, 1)], shifted[1], nc.gpsimd, 18)
         for a in range(PASSES):
             round_part(first_gate[:, a * wide : (a + 1) * wide], GATE, a, 0, 2)
         quantize(GATE, first_pair, first_gate[:])
@@ -243,10 +248,10 @@ def tile_list_rgg_relu_kernel(tc, tab_words, tab_scales, wa_words, wa_scales, wb
         pick_words(TARGET, 1, 6)
         part_words(SOURCE, 1)
         part_words(TARGET, 1)
-        early_message = placed("early_message", [P, wide], BF16, None)
+        weighted = weighted_message(0, *units[0], 13)
+        early_message = placed("early_message", [P, wide], BF16, 14)
         round_part(early_message[:], MESSAGE, 0, 2, 2)
         quantize(MESSAGE, [(2, 0), (3, 0)], early_message[:])
-        weighted = weighted_message(0, *units[0], 12)
         za = open_gate(0, *units[0])
         out_windows[1] = placed("out_window1", [P, T], F32, 0)
         nc.gpsimd.memset(out_windows[1][:], 0.0)

@@ -57,7 +57,7 @@ def tile_list_rgg_relu_kernel(tc, tab_words, tab_scales, wa_words, wa_scales, wb
         word_window = keep.tile([P, T], I32, align_bytes=64)
         wa_codes = [keep.tile([P, PASSES, N // 2], I32, name=f"wa_codes{pair}", align_bytes=64) for pair in range(2)]
         wa_plane = keep.tile([P, PASSES, N // 4], I32, align_bytes=64)
-        shifted = [keep.tile([P, c * HALF // 4], I32, name=f"shifted{c}", align_bytes=64) for c in (3, 1)]
+        shifted = [keep.tile([P, c * HALF // 4], I32, name=f"shifted{k}", align_bytes=64) for k, c in enumerate((1, 2, 1))]
         out_windows = {0: keep.tile([P, T], F32, name="out_window0", align_bytes=64)}
         weight_rows = keep.tile([P, P], F32, align_bytes=64)
         edge_weight = keep.tile([P, J // P], F32)
@@ -88,8 +88,8 @@ def tile_list_rgg_relu_kernel(tc, tab_words, tab_scales, wa_words, wa_scales, wb
             words = wa_words.rearrange("a p n i -> p a (n i)").bitcast(I32)
             nc.sync.dma_start(out=wa_codes[pair][:], in_=words[:, :, pair * 2 * P : (pair + 1) * 2 * P])
 
-        nc.sync.dma_start(lists[TARGET][:], offs2)
         nc.sync.dma_start(lists[SOURCE][:], offs)
+        nc.sync.dma_start(lists[TARGET][:], offs2)
         scale_rows = tab_scales.bitcast(I32).rearrange("a (q r) c -> r q a c", r=4)
         for r in range(4):
             nc.sync.dma_start(out=scale_window[r:P:SHIFT, :], in_=scale_rows[r])
@@ -132,16 +132,13 @@ def tile_list_rgg_relu_kernel(tc, tab_words, tab_scales, wa_words, wa_scales, wb
         def list_halves(i, h, count=1):
             return lists[i][:, h * LIST_COLS : (h + count) * LIST_COLS]
 
-        def pick_scales(runs, moved, queue, at=None):
-            picked = placed(f"picked_scales{len(runs)}", [P, sum(count for i, h, count in runs) * HALF], U8, at)
-            first = 0
-            for i, h, count in runs:
-                nc.vector.tensor_copy(out=picked[:, first * HALF : (first + count) * HALF], in_=scale_window[:].bitcast(U8).indirect(list_halves(i, h, count)))
-                for k in range(count):
-                    cols = slice((first + k) * HALF, (first + k + 1) * HALF)
-                    picked_scales[i, h + k] = (picked[:, cols], moved[:].bitcast(U8)[:, cols])
-                first = first + count
+        def pick_scales(i, h, count, moved, queue, at=None):
+            picked = placed(f"picked_scales{i}_{h}", [P, count * HALF], U8, at)
+            nc.vector.tensor_copy(out=picked[:], in_=scale_window[:].bitcast(U8).indirect(list_halves(i, h, count)))
             queue.dma_start(out=moved[0:PLANE_ROWS], in_=picked[SHIFT : SHIFT + PLANE_ROWS].bitcast(I32))
+            for k in range(count):
+                cols = slice(k * HALF, (k + 1) * HALF)
+                picked_scales[i, h + k] = (picked[:, cols], moved[:].bitcast(U8)[:, cols])
 
         def pick_words(i, h, at=None):
             picked_words[i, h] = placed(f"picked_words{i}_{h}", [P, HALF], U32, at)
@@ -223,24 +220,25 @@ def tile_list_rgg_relu_kernel(tc, tab_words, tab_scales, wa_words, wa_scales, wb
         units = [(0, 0), (1, 0), (0, 1), (1, 1), (2, 0), (3, 0), (2, 1), (3, 1)]
         weighted_at = {1: 28, 2: 38, 3: 40}
 
-        pick_scales([(TARGET, 0, 2), (SOURCE, 0, 1)], shifted[0], nc.sync)
         load_wa(0)
-        load_pair(MESSAGE, 0, 1)
-        pick_words(SOURCE, 0)
+        pick_scales(SOURCE, 0, 1, shifted[0], nc.gpsimd)
+        pick_scales(TARGET, 0, 2, shifted[1], nc.gpsimd)
+        pick_words(SOURCE, 0, 32)
         pick_words(TARGET, 0)
         part_words(SOURCE, 0)
+        load_pair(MESSAGE, 0, 1, 32)
         first_message = placed("first_message", [P, PASSES * wide], BF16, 16)
         first_gate = placed("first_gate", [P, PASSES * wide], BF16, 6)
         for a in range(PASSES):
             round_part(first_message[:, a * wide : (a + 1) * wide], MESSAGE, a, 0, 2)
         nc.scalar.copy(out=edge_weight[:], in_=turned_rows[:, 0 : J // P])
+        quantize(MESSAGE, first_pair, first_message[:])
+        part_words(TARGET, 0, 16)
+        pick_scales(SOURCE, 1, 1, shifted[2], nc.sync, 18)
         load_pair(MESSAGE, 1, 1)
         load_pair(GATE, 0, 1)
         load_pair(GATE, 1, 1)
         load_wa(1)
-        quantize(MESSAGE, first_pair, first_message[:])
-        part_words(TARGET, 0, 16)
-        pick_scales([(SOURCE, 1, 1)], shifted[1], nc.gpsimd, 18)
         for a in range(PASSES):
             round_part(first_gate[:, a * wide : (a + 1) * wide], GATE, a, 0, 2)
         quantize(GATE, first_pair, first_gate[:])
@@ -249,11 +247,11 @@ def tile_list_rgg_relu_kernel(tc, tab_words, tab_scales, wa_words, wa_scales, wb
         part_words(SOURCE, 1)
         part_words(TARGET, 1)
         weighted = weighted_message(0, *units[0], 13)
-        early_message = placed("early_message", [P, wide], BF16, 14)
+        early_message = placed("early_message", [P, wide], BF16, 12)
         round_part(early_message[:], MESSAGE, 0, 2, 2)
         quantize(MESSAGE, [(2, 0), (3, 0)], early_message[:])
         za = open_gate(0, *units[0])
-        out_windows[1] = placed("out_window1", [P, T], F32, 0)
+        out_windows[1] = placed("out_window1", [P, T], F32, 5)
         nc.gpsimd.memset(out_windows[1][:], 0.0)
         for u, (n, h) in enumerate(units):
             gate = close_gate(za, n, h)
@@ -270,4 +268,4 @@ def tile_list_rgg_relu_kernel(tc, tab_words, tab_scales, wa_words, wa_scales, wb
                     nc.gpsimd.memset(out_windows[2][:], 0.0)
             if u + 1 < len(units):
                 za = open_gate(u + 1, *units[u + 1])
-                weighted = weighted_message(u + 1, *units[u + 1], 12 if u == 0 else None, weighted_at.get(u + 1))
+                weighted = weighted_message(u + 1, *units[u + 1], 14 if u == 0 else None, weighted_at.get(u + 1))

@@ -16,6 +16,7 @@ FP8X4 = mybir.dt.float8_e4m3fn_x4
 FP4X4 = mybir.dt.float4_e2m1fn_x4
 MULT = mybir.AluOpType.mult
 SIGMOID = mybir.ActivationFunctionType.Sigmoid
+ADD = mybir.AluOpType.add
 RELU = mybir.ActivationFunctionType.Relu
 COPY = mybir.ActivationFunctionType.Copy
 
@@ -114,12 +115,12 @@ def tile_list_rgg_relu_kernel(tc, tab_words, tab_scales, wa_words, wa_scales, wb
         picked_words = {}
         parted = {}
 
-        def quantize(w, parts, rounded):
-            name = f"{w}_{parts[0][0]}_{parts[0][1]}"
+        def quantize(parts, rounded):
+            name = "_".join(str(x) for x in parts[0])
             words = keep.tile([P, len(parts) * P], U32, name=f"codes{name}", align_bytes=64)
             plane = keep.tile([P, len(parts) * P], U8, name=f"plane{name}", align_bytes=64)
             nc.vector.quantize_mx(out=words[:].bitcast(FP8X4), scales=plane[:], in_=rounded)
-            for k, (n, a) in enumerate(parts):
+            for k, (w, n, a) in enumerate(parts):
                 codes[w, n, a] = words[:, k * P : (k + 1) * P].bitcast(FP8X4)
                 planes[w, n, a] = plane[:, k * P : (k + 1) * P]
 
@@ -216,9 +217,9 @@ def tile_list_rgg_relu_kernel(tc, tab_words, tab_scales, wa_words, wa_scales, wb
 
         wide = 2 * K_PASS
         first_pair = [(n, a) for a in range(PASSES) for n in (0, 1)]
-        late_parts = {1: (MESSAGE, [(2, 1), (3, 1)]), 2: (GATE, [(2, 0), (2, 1)]), 3: (GATE, [(3, 0), (3, 1)])}
+        late_parts = {0: [(MESSAGE, 2, 1), (MESSAGE, 3, 1)], 1: [(GATE, 2, 0), (GATE, 2, 1)], 2: [(GATE, 3, 0), (GATE, 3, 1)]}
         units = [(0, 0), (1, 0), (0, 1), (1, 1), (2, 0), (3, 0), (2, 1), (3, 1)]
-        weighted_at = {1: 28, 2: 38, 3: 40}
+        weighted_at = {0: 28, 1: 36, 2: 38}
 
         load_wa(0)
         pick_scales(SOURCE, 0, 1, shifted[0], nc.gpsimd)
@@ -232,38 +233,42 @@ def tile_list_rgg_relu_kernel(tc, tab_words, tab_scales, wa_words, wa_scales, wb
         for a in range(PASSES):
             round_part(first_message[:, a * wide : (a + 1) * wide], MESSAGE, a, 0, 2)
         nc.scalar.copy(out=edge_weight[:], in_=turned_rows[:, 0 : J // P])
-        quantize(MESSAGE, first_pair, first_message[:])
+        quantize([(MESSAGE, n, a) for n, a in first_pair], first_message[:])
         part_words(TARGET, 0, 16)
-        pick_scales(SOURCE, 1, 1, shifted[2], nc.sync, 18)
         load_pair(MESSAGE, 1, 1)
+        pick_scales(SOURCE, 1, 1, shifted[2], nc.sync, 18)
         load_pair(GATE, 0, 1)
         load_pair(GATE, 1, 1)
         load_wa(1)
         for a in range(PASSES):
             round_part(first_gate[:, a * wide : (a + 1) * wide], GATE, a, 0, 2)
-        quantize(GATE, first_pair, first_gate[:])
-        pick_words(SOURCE, 1, 8)
-        pick_words(TARGET, 1, 6)
+        quantize([(GATE, n, a) for n, a in first_pair], first_gate[:])
+        pick_words(SOURCE, 1, 9)
+        pick_words(TARGET, 1, 5)
+        early_message = placed("early_message", [P, wide], BF16, 7)
+        nc.gpsimd.tensor_scalar(
+            early_message[:].rearrange("p (c i) -> p c i", i=PACK),
+            raw[MESSAGE, 0, 1][:].rearrange("p i c -> p c i"),
+            1.0, 0.0, MULT, ADD,
+        )
         part_words(SOURCE, 1)
         part_words(TARGET, 1)
-        weighted = weighted_message(0, *units[0], 13)
-        early_message = placed("early_message", [P, wide], BF16, 12)
-        round_part(early_message[:], MESSAGE, 0, 2, 2)
-        quantize(MESSAGE, [(2, 0), (3, 0)], early_message[:])
+        quantize([(MESSAGE, 2, 0), (MESSAGE, 3, 0)], early_message[:])
+        weighted = weighted_message(0, *units[0], 13, weighted_at[0])
         za = open_gate(0, *units[0])
-        out_windows[1] = placed("out_window1", [P, T], F32, 5)
+        out_windows[1] = placed("out_window1", [P, T], F32, 1)
         nc.gpsimd.memset(out_windows[1][:], 0.0)
         for u, (n, h) in enumerate(units):
             gate = close_gate(za, n, h)
             message = turn_message(u, weighted)
             scatter(n, h, gate, message)
             if u in weighted_at:
-                late = placed(f"late{u}", [P, wide], BF16, weighted_at[u])
-                w, parts = late_parts[u]
-                for k, (tile_n, a) in enumerate(parts):
+                parts = late_parts[u]
+                late = placed(f"late{u}", [P, len(parts) * K_PASS], BF16, weighted_at[u])
+                for k, (w, tile_n, a) in enumerate(parts):
                     round_part(late[:, k * K_PASS : (k + 1) * K_PASS], w, a, tile_n, 1)
-                quantize(w, parts, late[:])
-                if u == 1:
+                quantize(parts, late[:])
+                if u == 0:
                     out_windows[2] = placed("out_window2", [P, T], F32, 22)
                     nc.gpsimd.memset(out_windows[2][:], 0.0)
             if u + 1 < len(units):

@@ -48,7 +48,7 @@ def tile_list_rgg_relu_kernel(tc, tab_words, tab_scales, wa_words, wa_scales, wb
         def placed(name, shape, dtype, at):
             if at is None:
                 return keep.tile(shape, dtype, name=name, align_bytes=64)
-            return relay.tile(shape, dtype, name=name, offset=at * KIB, align_bytes=64)
+            return relay.tile(shape, dtype, name=name, offset=int(at * KIB), align_bytes=64)
 
         GATE, MESSAGE = 0, 1
         SOURCE, TARGET = 0, 1
@@ -90,10 +90,10 @@ def tile_list_rgg_relu_kernel(tc, tab_words, tab_scales, wa_words, wa_scales, wb
             nc.sync.dma_start(out=wa_codes[pair][:], in_=words[:, :, pair * 2 * P : (pair + 1) * 2 * P])
 
         nc.sync.dma_start(lists[SOURCE][:], offs)
-        nc.sync.dma_start(lists[TARGET][:], offs2)
         scale_rows = tab_scales.bitcast(I32).rearrange("a (q r) c -> r q a c", r=4)
         for r in range(4):
             nc.sync.dma_start(out=scale_window[r:P:SHIFT, :], in_=scale_rows[r])
+        nc.sync.dma_start(lists[TARGET][:], offs2)
         nc.sync.dma_start(out=word_window[:], in_=tab_words[0].rearrange("p t b -> p (t b)").bitcast(I32))
         load_pair(MESSAGE, 0, 0)
         nc.sync.dma_start(out=weight_rows[0 : J // P, :], in_=wgo[0].rearrange("(c p) -> c p", p=P))
@@ -102,9 +102,9 @@ def tile_list_rgg_relu_kernel(tc, tab_words, tab_scales, wa_words, wa_scales, wb
                 out=wa_plane[32 * q : 32 * q + 4, :, :],
                 in_=wa_scales[:, 4 * q : 4 * q + 4, :].bitcast(I32).rearrange("a r c -> r a c"),
             )
-        load_pair(MESSAGE, 1, 0)
+        load_pair(MESSAGE, 1, 0, 40)
         load_pair(GATE, 0, 0)
-        load_pair(GATE, 1, 0, 12)
+        load_pair(GATE, 1, 0, 48)
 
         turned_rows = bank("turned_rows", [P, HALF], 6)
         nc.tensor.transpose(turned_rows[:, 0:P], weight_rows[:], identity[:])
@@ -234,17 +234,17 @@ def tile_list_rgg_relu_kernel(tc, tab_words, tab_scales, wa_words, wa_scales, wb
             round_part(first_message[:, a * wide : (a + 1) * wide], MESSAGE, a, 0, 2)
         nc.scalar.copy(out=edge_weight[:], in_=turned_rows[:, 0 : J // P])
         quantize([(MESSAGE, n, a) for n, a in first_pair], first_message[:])
-        part_words(TARGET, 0, 16)
+        part_words(TARGET, 0, 40)
         load_pair(MESSAGE, 1, 1)
-        pick_scales(SOURCE, 1, 1, shifted[2], nc.sync, 18)
+        pick_scales(SOURCE, 1, 1, shifted[2], nc.sync, 42)
         load_pair(GATE, 0, 1)
         load_pair(GATE, 1, 1)
         load_wa(1)
         for a in range(PASSES):
             round_part(first_gate[:, a * wide : (a + 1) * wide], GATE, a, 0, 2)
         quantize([(GATE, n, a) for n, a in first_pair], first_gate[:])
-        pick_words(SOURCE, 1, 9)
-        pick_words(TARGET, 1, 5)
+        pick_words(SOURCE, 1, 46.5)
+        pick_words(TARGET, 1, 48.5)
         early_message = placed("early_message", [P, wide], BF16, 7)
         nc.gpsimd.tensor_scalar(
             early_message[:].rearrange("p (c i) -> p c i", i=PACK),
@@ -254,7 +254,7 @@ def tile_list_rgg_relu_kernel(tc, tab_words, tab_scales, wa_words, wa_scales, wb
         part_words(SOURCE, 1)
         part_words(TARGET, 1)
         quantize([(MESSAGE, 2, 0), (MESSAGE, 3, 0)], early_message[:])
-        weighted = weighted_message(0, *units[0], 13, weighted_at[0])
+        weighted = weighted_message(0, *units[0], 51, weighted_at[0])
         za = open_gate(0, *units[0])
         out_windows[1] = placed("out_window1", [P, T], F32, 1)
         nc.gpsimd.memset(out_windows[1][:], 0.0)
@@ -273,4 +273,4 @@ def tile_list_rgg_relu_kernel(tc, tab_words, tab_scales, wa_words, wa_scales, wb
                     nc.gpsimd.memset(out_windows[2][:], 0.0)
             if u + 1 < len(units):
                 za = open_gate(u + 1, *units[u + 1])
-                weighted = weighted_message(u + 1, *units[u + 1], 14 if u == 0 else None, weighted_at.get(u + 1))
+                weighted = weighted_message(u + 1, *units[u + 1], 52 if u == 0 else None, weighted_at.get(u + 1))

@@ -213,7 +213,11 @@ def tile_list_rgg_relu_kernel(tc, tab_words, tab_scales, wa_words, wa_scales, wb
             window = out_windows[n % 3]
             nc.vector.tensor_tensor(window[:].indirect(list_halves(TARGET, h)), message[:], gate[:], MULT)
             if h == HALVES - 1:
-                nc.sync.dma_start(out=out[n * P : (n + 1) * P, :], in_=window[:])
+                queues = (nc.sync, nc.scalar) if n == N // P - 1 else (nc.sync,)
+                width = T // len(queues)
+                for k, queue in enumerate(queues):
+                    cols = slice(k * width, (k + 1) * width)
+                    queue.dma_start(out=out[n * P : (n + 1) * P, cols], in_=window[:, cols])
 
         wide = 2 * K_PASS
         first_pair = [(n, a) for a in range(PASSES) for n in (0, 1)]

@@ -221,9 +221,9 @@ def tile_list_rgg_relu_kernel(tc, tab_words, tab_scales, wa_words, wa_scales, wb
 
         wide = 2 * K_PASS
         first_pair = [(n, a) for a in range(PASSES) for n in (0, 1)]
-        late_parts = {0: [(MESSAGE, 2, 1), (MESSAGE, 3, 1)], 1: [(GATE, 2, 0), (GATE, 2, 1)], 2: [(GATE, 3, 0), (GATE, 3, 1)]}
+        late_parts = {1: [(MESSAGE, 2, 1), (MESSAGE, 3, 1)], 2: [(GATE, 2, 0), (GATE, 2, 1), (GATE, 3, 0), (GATE, 3, 1)]}
         units = [(0, 0), (1, 0), (0, 1), (1, 1), (2, 0), (3, 0), (2, 1), (3, 1)]
-        weighted_at = {0: 28, 1: 36, 2: 38}
+        weighted_at = {1: 28, 2: 56}
 
         load_wa(0)
         pick_scales(SOURCE, 0, 1, shifted[0], nc.gpsimd)
@@ -258,7 +258,7 @@ def tile_list_rgg_relu_kernel(tc, tab_words, tab_scales, wa_words, wa_scales, wb
         part_words(SOURCE, 1)
         part_words(TARGET, 1)
         quantize([(MESSAGE, 2, 0), (MESSAGE, 3, 0)], early_message[:])
-        weighted = weighted_message(0, *units[0], 51, weighted_at[0])
+        weighted = weighted_message(0, *units[0], 51)
         za = open_gate(0, *units[0])
         out_windows[1] = placed("out_window1", [P, T], F32, 1)
         nc.gpsimd.memset(out_windows[1][:], 0.0)
@@ -272,7 +272,7 @@ def tile_list_rgg_relu_kernel(tc, tab_words, tab_scales, wa_words, wa_scales, wb
                 for k, (w, tile_n, a) in enumerate(parts):
                     round_part(late[:, k * K_PASS : (k + 1) * K_PASS], w, a, tile_n, 1)
                 quantize(parts, late[:])
-                if u == 0:
+                if u == 1:
                     out_windows[2] = placed("out_window2", [P, T], F32, 22)
                     nc.gpsimd.memset(out_windows[2][:], 0.0)
             if u + 1 < len(units):

@@ -156,7 +156,7 @@ def tile_list_rgg_relu_kernel(tc, tab_words, tab_scales, wa_words, wa_scales, wb
             return parted[i, h][:, a, 2 * first : 2 * (first + width)].bitcast(FP4X4), picked_scales[i, h][a][:, first : first + width]
 
         def weighted_message(u, n, h, positive_at=None, weighted_at=None):
-            mt = bank(f"mt{u}", [P, E_TILES, P], 4 if u < 2 else (u + 1) % 4)
+            mt = bank(f"mt{u}", [P, E_TILES, P], 4 if u < 2 else 5 if u == 5 else (u + 1) % 4)
             for e in range(E_TILES):
                 for a in range(PASSES):
                     words, plane = table_operand(SOURCE, h, a, e * P, P)
@@ -181,7 +181,7 @@ def tile_list_rgg_relu_kernel(tc, tab_words, tab_scales, wa_words, wa_scales, wb
 
         def open_gate(u, n, h):
             cols = slice(n * P, (n + 1) * P)
-            za = bank(f"za{u}", [P, HALF], 5)
+            za = bank(f"za{u}", [P, HALF], 3 if u == 5 else 5)
             for a in range(PASSES):
                 words, plane = table_operand(TARGET, h, a, 0, HALF)
                 nc.tensor.matmul_mx(

@@ -70,10 +70,10 @@ def tile_list_rgg_relu_kernel(tc, tab_words, tab_scales, wa_words, wa_scales, wb
         nc.scalar.activation(out=warm[:, 0:1], in_=warm[:, 1:2], func=SIGMOID)
         nc.gpsimd.memset(weight_rows[:], 0.0)
         nc.gpsimd.memset(wa_plane[:], 0)
+        nc.gpsimd.memset(out_windows[0][:], 0.0)
         make_identity(nc, identity[:])
         for tile in shifted:
             nc.gpsimd.memset(tile[:], 0)
-        nc.gpsimd.memset(out_windows[0][:], 0.0)
 
         raw = {}
 

@@ -156,7 +156,7 @@ def tile_list_rgg_relu_kernel(tc, tab_words, tab_scales, wa_words, wa_scales, wb
             return parted[i, h][:, a, 2 * first : 2 * (first + width)].bitcast(FP4X4), picked_scales[i, h][a][:, first : first + width]
 
         def weighted_message(u, n, h, positive_at=None, weighted_at=None):
-            mt = bank(f"mt{u}", [P, E_TILES, P], 4 if u < 2 else 5 if u == 5 else (u + 1) % 4)
+            mt = bank(f"mt{u}", [P, E_TILES, P], 4 if u == 0 else 7 if u == 1 else 5 if u == 5 else (u + 1) % 4)
             for e in range(E_TILES):
                 for a in range(PASSES):
                     words, plane = table_operand(SOURCE, h, a, e * P, P)

@@ -156,7 +156,7 @@ def tile_list_rgg_relu_kernel(tc, tab_words, tab_scales, wa_words, wa_scales, wb
             return parted[i, h][:, a, 2 * first : 2 * (first + width)].bitcast(FP4X4), picked_scales[i, h][a][:, first : first + width]
 
         def weighted_message(u, n, h, positive_at=None, weighted_at=None):
-            mt = bank(f"mt{u}", [P, E_TILES, P], 4 if u == 0 else 7 if u == 1 else 5 if u == 5 else (u + 1) % 4)
+            mt = bank(f"mt{u}", [P, E_TILES, P], 4 if u == 0 else 7 if u == 1 else 4 if u == 5 else (u + 1) % 4)
             for e in range(E_TILES):
                 for a in range(PASSES):
                     words, plane = table_operand(SOURCE, h, a, e * P, P)
@@ -181,7 +181,7 @@ def tile_list_rgg_relu_kernel(tc, tab_words, tab_scales, wa_words, wa_scales, wb
 
         def open_gate(u, n, h):
             cols = slice(n * P, (n + 1) * P)
-            za = bank(f"za{u}", [P, HALF], 3 if u == 5 else 5)
+            za = bank(f"za{u}", [P, HALF], 3 if u == 5 else 4)
             for a in range(PASSES):
                 words, plane = table_operand(TARGET, h, a, 0, HALF)
                 nc.tensor.matmul_mx(

from contextlib import ExitStack

import concourse.mybir as mybir
from concourse.masks import make_identity

K, N, T, J = 1024, 512, 2048, 1024
FLOPS = 2 * 3 * K * N * J

F32 = mybir.dt.float32
BF16 = mybir.dt.bfloat16
I32 = mybir.dt.int32
U32 = mybir.dt.uint32
U16 = mybir.dt.uint16
U8 = mybir.dt.uint8
FP8X4 = mybir.dt.float8_e4m3fn_x4
FP4X4 = mybir.dt.float4_e2m1fn_x4
MULT = mybir.AluOpType.mult
SIGMOID = mybir.ActivationFunctionType.Sigmoid
ADD = mybir.AluOpType.add
RELU = mybir.ActivationFunctionType.Relu
COPY = mybir.ActivationFunctionType.Copy

P = 128
PACK = 4
PASSES = 2
K_PASS = P * PACK
HALF = 512
HALVES = J // HALF
E_TILES = HALF // P
LIST_COLS = HALF // 16
KIB = 1024
BANK = 2 * KIB
SHIFT = 16
PLANE_ROWS = 100


def tile_list_rgg_relu_kernel(tc, tab_words, tab_scales, wa_words, wa_scales, wb, wc, wgo, offs, offs2, out):
    nc = tc.nc
    with ExitStack() as ctx:
        keep = ctx.enter_context(tc.tile_pool(name="keep", bufs=1))
        ring = ctx.enter_context(tc.tile_pool(name="ring", bufs=3))
        relay = ctx.enter_context(tc.tile_pool(name="relay", bufs=1))
        psum = ctx.enter_context(tc.psum_pool(name="psum", bufs=1))

        def bank(name, shape, index):
            return psum.tile(shape, F32, name=name, offset=index * BANK)

        def placed(name, shape, dtype, at):
            if at is None:
                return keep.tile(shape, dtype, name=name, align_bytes=64)
            return relay.tile(shape, dtype, name=name, offset=int(at * KIB), align_bytes=64)

        GATE, MESSAGE = 0, 1
        SOURCE, TARGET = 0, 1

        lists = [keep.tile([P, J // 16], U16, name=f"list{i}") for i in range(2)]
        scale_window = keep.tile([P, T // 4], I32, align_bytes=64)
        word_window = keep.tile([P, T], I32, align_bytes=64)
        wa_codes = [keep.tile([P, PASSES, N // 2], I32, name=f"wa_codes{pair}", align_bytes=64) for pair in range(2)]
        wa_plane = keep.tile([P, PASSES, N // 4], I32, align_bytes=64)
        shifted = [keep.tile([P, c * HALF // 4], I32, name=f"shifted{k}", align_bytes=64) for k, c in enumerate((1, 2, 1))]
        out_windows = {0: keep.tile([P, T], F32, name="out_window0", align_bytes=64)}
        weight_rows = keep.tile([P, P], F32, align_bytes=64)
        edge_weight = keep.tile([P, J // P], F32)
        identity = keep.tile([P, P], F32, align_bytes=64)
        warm = keep.tile([P, 8], F32)

        nc.gpsimd.memset(scale_window[:], 0)
        nc.gpsimd.memset(warm[:], 0.0)
        nc.scalar.activation(out=warm[:, 0:1], in_=warm[:, 1:2], func=SIGMOID)
        nc.gpsimd.memset(weight_rows[:], 0.0)
        nc.gpsimd.memset(wa_plane[:], 0)
        nc.gpsimd.memset(out_windows[0][:], 0.0)
        make_identity(nc, identity[:])
        for tile in shifted:
            nc.gpsimd.memset(tile[:], 0)

        raw = {}

        def load_pair(w, a, pair, at=None):
            t = placed(f"raw{w}_{a}_{pair}", [P, PACK, 2 * P], F32, at)
            nc.sync.dma_start(
                out=t[:],
                in_=(wb, wc)[w][a * K_PASS : (a + 1) * K_PASS, pair * 2 * P : (pair + 1) * 2 * P].rearrange("(p i) n -> p i n", i=PACK),
            )
            raw[w, a, pair] = t

        def load_wa(pair):
            words = wa_words.rearrange("a p n i -> p a (n i)").bitcast(I32)
            nc.sync.dma_start(out=wa_codes[pair][:], in_=words[:, :, pair * 2 * P : (pair + 1) * 2 * P])

        nc.sync.dma_start(lists[SOURCE][:], offs)
        scale_rows = tab_scales.bitcast(I32).rearrange("a (q r) c -> r q a c", r=4)
        for r in range(4):
            nc.sync.dma_start(out=scale_window[r:P:SHIFT, :], in_=scale_rows[r])
        nc.sync.dma_start(lists[TARGET][:], offs2)
        nc.sync.dma_start(out=word_window[:], in_=tab_words[0].rearrange("p t b -> p (t b)").bitcast(I32))
        load_pair(MESSAGE, 0, 0)
        nc.sync.dma_start(out=weight_rows[0 : J // P, :], in_=wgo[0].rearrange("(c p) -> c p", p=P))
        for q in range(4):
            nc.sync.dma_start(
                out=wa_plane[32 * q : 32 * q + 4, :, :],
                in_=wa_scales[:, 4 * q : 4 * q + 4, :].bitcast(I32).rearrange("a r c -> r a c"),
            )
        load_pair(MESSAGE, 1, 0, 40)
        load_pair(GATE, 0, 0)
        load_pair(GATE, 1, 0, 48)

        turned_rows = bank("turned_rows", [P, HALF], 6)
        nc.tensor.transpose(turned_rows[:, 0:P], weight_rows[:], identity[:])

        codes = {}
        planes = {}
        picked_scales = {}
        picked_words = {}
        parted = {}

        def quantize(parts, rounded):
            name = "_".join(str(x) for x in parts[0])
            words = keep.tile([P, len(parts) * P], U32, name=f"codes{name}", align_bytes=64)
            plane = keep.tile([P, len(parts) * P], U8, name=f"plane{name}", align_bytes=64)
            nc.vector.quantize_mx(out=words[:].bitcast(FP8X4), scales=plane[:], in_=rounded)
            for k, (w, n, a) in enumerate(parts):
                codes[w, n, a] = words[:, k * P : (k + 1) * P].bitcast(FP8X4)
                planes[w, n, a] = plane[:, k * P : (k + 1) * P]

        def round_part(dst, w, a, first, count):
            nc.scalar.copy(
                out=dst.rearrange("p (n c m i) -> p n c i m", n=count, m=4, i=PACK),
                in_=raw[w, a, first // 2][:, :, first % 2 * P : (first % 2 + count) * P].rearrange("p i (n c m) -> p n c i m", n=count, m=4),
            )

        def list_halves(i, h, count=1):
            return lists[i][:, h * LIST_COLS : (h + count) * LIST_COLS]

        def pick_scales(i, h, count, moved, queue, at=None):
            picked = placed(f"picked_scales{i}_{h}", [P, count * HALF], U8, at)
            nc.vector.tensor_copy(out=picked[:], in_=scale_window[:].bitcast(U8).indirect(list_halves(i, h, count)))
            queue.dma_start(out=moved[0:PLANE_ROWS], in_=picked[SHIFT : SHIFT + PLANE_ROWS].bitcast(I32))
            for k in range(count):
                cols = slice(k * HALF, (k + 1) * HALF)
                picked_scales[i, h + k] = (picked[:, cols], moved[:].bitcast(U8)[:, cols])

        def pick_words(i, h, at=None):
            picked_words[i, h] = placed(f"picked_words{i}_{h}", [P, HALF], U32, at)
            nc.vector.tensor_copy(out=picked_words[i, h][:], in_=word_window[:].bitcast(U32).indirect(list_halves(i, h)))

        def part_words(i, h, at=None):
            parted[i, h] = placed(f"parted{i}_{h}", [P, PASSES, 2 * HALF], U8, at)
            nc.vector.tensor_copy(
                out=parted[i, h][:].bitcast(U16),
                in_=picked_words[i, h][:].bitcast(U16).rearrange("p (j d) -> p d j", d=PASSES),
            )

        def table_operand(i, h, a, first, width):
            return parted[i, h][:, a, 2 * first : 2 * (first + width)].bitcast(FP4X4), picked_scales[i, h][a][:, first : first + width]

        def weighted_message(u, n, h, positive_at=None, weighted_at=None):
            mt = bank(f"mt{u}", [P, E_TILES, P], 4 if u == 0 else 7 if u == 1 else 4 if u == 5 else (u + 1) % 4)
            for e in range(E_TILES):
                for a in range(PASSES):
                    words, plane = table_operand(SOURCE, h, a, e * P, P)
                    nc.tensor.matmul_mx(
                        out=mt[:, e, :], lhsT=words, lhsT_scale=plane,
                        rhs=codes[MESSAGE, n, a], rhs_scale=planes[MESSAGE, n, a],
                        start=(a == 0), stop=(a == PASSES - 1),
                    )
            if positive_at is None:
                positive = ring.tile([P, E_TILES, P], F32, name="positive")
            else:
                positive = placed(f"positive{u}", [P, E_TILES, P], F32, positive_at)
            nc.scalar.activation(out=positive[:], in_=mt[:], func=RELU)
            if weighted_at is None:
                weighted = ring.tile([P, E_TILES, P], F32, name="weighted", align_bytes=64)
            else:
                weighted = placed(f"weighted{u}", [P, E_TILES, P], F32, weighted_at)
            for e in range(E_TILES):
                c = h * E_TILES + e
                nc.scalar.activation(out=weighted[:, e, :], in_=positive[:, e, :], func=COPY, scale=edge_weight[:, c : c + 1])
            return weighted

        def open_gate(u, n, h):
            cols = slice(n * P, (n + 1) * P)
            za = bank(f"za{u}", [P, HALF], 3 if u == 5 else 4)
            for a in range(PASSES):
                words, plane = table_operand(TARGET, h, a, 0, HALF)
                nc.tensor.matmul_mx(
                    out=za[:], lhsT=wa_codes[n // 2][:, a, n % 2 * P : (n % 2 + 1) * P].bitcast(FP8X4), lhsT_scale=wa_plane[:, a, :].bitcast(U8)[:, cols],
                    rhs=words, rhs_scale=plane, start=(a == 0), stop=False,
                )
            return za

        def close_gate(za, n, h):
            for a in range(PASSES):
                words, plane = table_operand(SOURCE, h, a, 0, HALF)
                nc.tensor.matmul_mx(
                    out=za[:], lhsT=codes[GATE, n, a], lhsT_scale=planes[GATE, n, a],
                    rhs=words, rhs_scale=plane, start=False, stop=(a == PASSES - 1),
                )
            gate = ring.tile([P, HALF], F32, name="gate")
            nc.scalar.activation(out=gate[:], in_=za[:], func=SIGMOID)
            return gate

        def turn_message(u, weighted):
            turned = bank(f"turned{u}", [P, HALF], (u + 3) % 4)
            for e in range(E_TILES):
                nc.tensor.transpose(turned[:, e * P : (e + 1) * P], weighted[:, e, :], identity[:])
            message = ring.tile([P, HALF], F32, name="message")
            nc.scalar.copy(out=message[:], in_=turned[:])
            return message

        def scatter(n, h, gate, message):
            window = out_windows[n % 3]
            nc.vector.tensor_tensor(window[:].indirect(list_halves(TARGET, h)), message[:], gate[:], MULT)
            if h == HALVES - 1:
                queues = (nc.sync, nc.scalar) if n == N // P - 1 else (nc.sync,)
                width = T // len(queues)
                for k, queue in enumerate(queues):
                    cols = slice(k * width, (k + 1) * width)
                    queue.dma_start(out=out[n * P : (n + 1) * P, cols], in_=window[:, cols])

        wide = 2 * K_PASS
        first_pair = [(n, a) for a in range(PASSES) for n in (0, 1)]
        late_parts = {1: [(MESSAGE, 2, 1), (MESSAGE, 3, 1)], 2: [(GATE, 2, 0), (GATE, 2, 1), (GATE, 3, 0), (GATE, 3, 1)]}
        units = [(0, 0), (1, 0), (0, 1), (1, 1), (2, 0), (3, 0), (2, 1), (3, 1)]
        weighted_at = {1: 28, 2: 56}

        load_wa(0)
        pick_scales(SOURCE, 0, 1, shifted[0], nc.gpsimd)
        pick_scales(TARGET, 0, 2, shifted[1], nc.gpsimd)
        pick_words(SOURCE, 0, 32)
        pick_words(TARGET, 0)
        part_words(SOURCE, 0)
        load_pair(MESSAGE, 0, 1, 32)
        first_message = placed("first_message", [P, PASSES * wide], BF16, 16)
        first_gate = placed("first_gate", [P, PASSES * wide], BF16, 6)
        for a in range(PASSES):
            round_part(first_message[:, a * wide : (a + 1) * wide], MESSAGE, a, 0, 2)
        nc.scalar.copy(out=edge_weight[:], in_=turned_rows[:, 0 : J // P])
        quantize([(MESSAGE, n, a) for n, a in first_pair], first_message[:])
        part_words(TARGET, 0, 40)
        load_pair(MESSAGE, 1, 1)
        pick_scales(SOURCE, 1, 1, shifted[2], nc.sync, 42)
        load_pair(GATE, 0, 1)
        load_pair(GATE, 1, 1)
        load_wa(1)
        for a in range(PASSES):
            round_part(first_gate[:, a * wide : (a + 1) * wide], GATE, a, 0, 2)
        quantize([(GATE, n, a) for n, a in first_pair], first_gate[:])
        pick_words(SOURCE, 1, 46.5)
        pick_words(TARGET, 1, 48.5)
        early_message = placed("early_message", [P, wide], BF16, 7)
        nc.gpsimd.tensor_scalar(
            early_message[:].rearrange("p (c i) -> p c i", i=PACK),
            raw[MESSAGE, 0, 1][:].rearrange("p i c -> p c i"),
            1.0, 0.0, MULT, ADD,
        )
        part_words(SOURCE, 1)
        part_words(TARGET, 1)
        quantize([(MESSAGE, 2, 0), (MESSAGE, 3, 0)], early_message[:])
        weighted = weighted_message(0, *units[0], 51)
        za = open_gate(0, *units[0])
        out_windows[1] = placed("out_window1", [P, T], F32, 1)
        nc.gpsimd.memset(out_windows[1][:], 0.0)
        for u, (n, h) in enumerate(units):
            gate = close_gate(za, n, h)
            message = turn_message(u, weighted)
            scatter(n, h, gate, message)
            if u in weighted_at:
                parts = late_parts[u]
                late = placed(f"late{u}", [P, len(parts) * K_PASS], BF16, weighted_at[u])
                for k, (w, tile_n, a) in enumerate(parts):
                    round_part(late[:, k * K_PASS : (k + 1) * K_PASS], w, a, tile_n, 1)
                quantize(parts, late[:])
                if u == 1:
                    out_windows[2] = placed("out_window2", [P, T], F32, 22)
                    nc.gpsimd.memset(out_windows[2][:], 0.0)
            if u + 1 < len(units):
                za = open_gate(u + 1, *units[u + 1])
                weighted = weighted_message(u + 1, *units[u + 1], 52 if u == 0 else None, weighted_at.get(u + 1))
